import numpy as np
import ml_dtypes


def mxq(x, axis, fmt="e4m3"):
    dtype, down = {"e4m3": (ml_dtypes.float8_e4m3fn, 7), "e5m2": (ml_dtypes.float8_e5m2, 14)}[fmt]
    v = np.moveaxis(np.asarray(x, np.float32).astype(ml_dtypes.bfloat16).astype(np.float64), axis, -1)
    blocks = v.reshape(v.shape[:-1] + (-1, 32))
    amax = np.abs(blocks).max(-1, keepdims=True)
    byte = np.maximum(np.where(amax > 0, np.frexp(amax)[1] - 1 + 127, 0) - down, 1)
    scale = np.exp2(byte - 127.0)
    codes = (blocks / scale).astype(np.float32).astype(dtype).astype(np.float64)
    return np.moveaxis((codes * scale).reshape(v.shape), -1, axis)


WIDE = False


def mx_kscale(k):
    if not WIDE:
        return np.ones(k)
    levels = np.array([10, -10, 5, -5, 0])
    if k % 512:
        return np.exp2(np.random.permutation(np.resize(levels, k // 32))).repeat(32)
    a = np.empty((k // 512, 16))
    for p in range(k // 512):
        a[p, :8] = np.random.permutation(np.resize(levels, 8))
        for g in range(8):
            far = levels[np.abs(levels - a[p, g]) >= 10]
            a[p, g + 8] = far[np.random.randint(len(far))]
    return np.exp2(a.ravel()).repeat(32)


def f64(x):
    return np.asarray(x).astype(np.float64)


def striped8(idx):
    return np.concatenate([x.reshape(-1, 16).T for x in idx]).astype(np.uint16)


def runs(offs, k):
    lists = np.stack([offs[16 * r : 16 * r + 16].T.reshape(-1) for r in range(8)]).astype(np.int64)
    return lists[np.arange(k) % 512 // 64]


def pack_weight(w):
    k, n = w.shape
    w = f64(np.asarray(w, np.float32).astype(ml_dtypes.bfloat16)).reshape(k // 32, 32, n)
    amax = np.abs(w).max(1)
    byte = np.clip(np.where(amax > 0, np.frexp(amax)[1] - 1 + 127 - 7, 1), 1, 254)
    scaled = (w * np.exp2(127.0 - byte)[:, None, :]).reshape(k, n).astype(np.float32)
    words = np.ascontiguousarray(scaled.reshape(k // 512, 128, 4, n).transpose(0, 1, 3, 2)).astype(ml_dtypes.float8_e4m3fn).view(np.uint8)
    return words, np.ascontiguousarray(byte.astype(np.uint8).reshape(k // 512, 16, n))


def unpack_weight(words, scales):
    g, p, n, _ = words.shape
    vals = np.ascontiguousarray(words).view(ml_dtypes.float8_e4m3fn).astype(np.float64) * np.repeat(np.exp2(scales.astype(np.float64) - 127.0), 8, axis=1)[..., None]
    return vals.transpose(0, 1, 3, 2).reshape(g * 512, n)


def gelu(v):
    return 0.5 * v * (1.0 + np.tanh(np.sqrt(2.0 / np.pi) * (v + 0.044715 * v**3)))


K, T, S, H, N = 512, 2048, 1024, 512, 256


def setup_inputs():
    n = np.random.standard_normal
    s = mx_kscale(K)[:, None]
    u = mx_kscale(H)
    packed_xT = pack_weight(n((K, T)) * s)
    packed_w2 = pack_weight(n((H, N)) / np.sqrt(H) / u[:, None])
    return {
        "x_words": packed_xT[0],
        "x_scales": packed_xT[1],
        "w1": (n((K, H)) / np.sqrt(K) / s * u).astype(np.float32),
        "w2_words": packed_w2[0],
        "w2_scales": packed_w2[1],
        "offs": striped8(np.stack([np.random.permutation(T)[:S] for _ in range(8)])),
    }


def reference(x_words, x_scales, w1, w2_words, w2_scales, offs):
    xq = unpack_weight(x_words, x_scales)[np.arange(K)[:, None], runs(offs, K)]
    h = gelu(mxq(f64(w1), 0, "e4m3").T @ xq)
    return unpack_weight(w2_words, w2_scales).T @ mxq(h, 0, "e4m3")

@@ -1,0 +1,139 @@
+from contextlib import ExitStack
+
+import concourse.mybir as mybir
+
+K, T, S, H, N = 512, 2048, 1024, 512, 256
+FLOPS = 2 * S * (K * H + H * N)
+
+F32 = mybir.dt.float32
+BF16 = mybir.dt.bfloat16
+I32 = mybir.dt.int32
+U32 = mybir.dt.uint32
+U16 = mybir.dt.uint16
+U8 = mybir.dt.uint8
+FP8X4 = mybir.dt.float8_e4m3fn_x4
+GELU = mybir.ActivationFunctionType.Gelu_apprx_tanh
+
+P = 128
+PACK = 4
+BLOCK = 128
+WORD_GATHERS = (256, 256, 512)
+OUT_GROUPS = (128,) * 8
+
+
+def tile_picked_phmlp_gelu_p_kernel(tc, x_words, x_scales, w1, w2_words, w2_scales, offs, out):
+    nc = tc.nc
+    with ExitStack() as ctx:
+        keep = ctx.enter_context(tc.tile_pool(name="keep", bufs=1))
+        psum_h = ctx.enter_context(tc.psum_pool(name="psum_h", bufs=4))
+        psum_o = ctx.enter_context(tc.psum_pool(name="psum_o", bufs=4))
+
+        offsets = keep.tile([P, S // 16], U16, name="offsets")
+        nc.sync.dma_start(offsets[:], offs)
+
+        scale_window = keep.tile([P, T], U8, name="scale_window", align_bytes=64)
+        nc.sync.dma_start(scale_window[:].bitcast(I32), x_scales[0].bitcast(I32).unsqueeze(1).to_broadcast([16, 8, T // 4]))
+
+        x_plane = keep.tile([P, S], U8, name="x_plane", align_bytes=64)
+        nc.vector.memset(x_plane[:].bitcast(I32), 0)
+        warm = keep.tile([P, 8], F32, name="warm")
+        nc.vector.memset(warm[:, 0:1], 0.0)
+        nc.scalar.activation(warm[:, 4:5], warm[:, 0:1], GELU)
+
+        w1_rows = w1.rearrange("(p j) c -> p j c", j=PACK)
+        w1_raw = []
+        for half in range(2):
+            raw = keep.tile([P, PACK, H // 2], F32, name=f"w1_raw{half}")
+            nc.sync.dma_start(raw[:], w1_rows[:, :, half * (H // 2) : (half + 1) * (H // 2)])
+            w1_raw.append(raw)
+
+        w2_plane = keep.tile([P, N], U8, name="w2_plane", align_bytes=64)
+        for q in range(4):
+            nc.sync.dma_start(
+                w2_plane[32 * q : 32 * q + 32, :].bitcast(I32),
+                w2_scales[0, 4 * q : 4 * q + 4, :].bitcast(I32).unsqueeze(0).to_broadcast([8, 4, N // 4]),
+            )
+
+        word_window = keep.tile([P, T], U32, name="word_window", align_bytes=64)
+        nc.sync.dma_start(word_window[:].bitcast(I32), x_words[0].rearrange("p n t -> p (n t)").bitcast(I32))
+
+        w2_codes = keep.tile([P, N], U32, name="w2_codes", align_bytes=64)
+        nc.sync.dma_start(w2_codes[:].bitcast(I32), w2_words[0].rearrange("p n t -> p (n t)").bitcast(I32))
+
+        picked_scales = keep.tile([P, S], U8, name="picked_scales", align_bytes=64)
+        nc.vector.tensor_copy(picked_scales[:], scale_window[:].indirect(offsets[:]))
+        for q in range(4):
+            nc.sync.dma_start(x_plane[32 * q : 32 * q + 4, :].bitcast(I32), picked_scales[32 * q : 32 * q + 32 : 8, :].bitcast(I32))
+
+        w1_grouped = keep.tile([P, H * PACK], BF16, name="w1_grouped", align_bytes=64)
+        grouped_view = w1_grouped[:].rearrange("p (t m j) -> p m t j", t=PACK, j=PACK)
+        for half in range(2):
+            nc.scalar.copy(grouped_view[:, half * 64 : (half + 1) * 64], w1_raw[half][:].rearrange("p j (m t) -> p m t j", t=PACK))
+        w1_codes = keep.tile([P, H], U32, name="w1_codes", align_bytes=64)
+        w1_plane = keep.tile([P, H], U8, name="w1_plane", align_bytes=64)
+        nc.vector.quantize_mx(out=w1_codes[:].bitcast(FP8X4), scales=w1_plane[:], in_=w1_grouped[:])
+
+        picked_words = keep.tile([P, S], U32, name="picked_words", align_bytes=64)
+        start = 0
+        for width in WORD_GATHERS:
+            nc.vector.tensor_copy(
+                picked_words[:, start : start + width],
+                word_window[:].indirect(offsets[:, start // 16 : (start + width) // 16]),
+            )
+            start = start + width
+
+        out_rows = out.rearrange("(h p) n -> p h n", p=P)
+        start = 0
+        for g, width in enumerate(OUT_GROUPS):
+            hidden = keep.tile([P, width * PACK], BF16, name=f"hidden{g}", align_bytes=64)
+            for b in range(width // BLOCK):
+                cols = slice(start + b * BLOCK, start + (b + 1) * BLOCK)
+                pre = psum_h.tile([P, PACK, BLOCK], F32, name="pre")
+                for t in range(PACK):
+                    nc.tensor.matmul_mx(
+                        out=pre[:, t, :],
+                        lhsT=w1_codes[:, t * P : (t + 1) * P].bitcast(FP8X4),
+                        lhsT_scale=w1_plane[:, t * P : (t + 1) * P],
+                        rhs=picked_words[:, cols].bitcast(FP8X4),
+                        rhs_scale=x_plane[:, cols],
+                        start=True,
+                        stop=True,
+                    )
+                nc.scalar.activation(
+                    hidden[:, b * BLOCK * PACK : (b + 1) * BLOCK * PACK].rearrange("p (n t) -> p n t", t=PACK),
+                    pre[:].rearrange("p t n -> p n t"),
+                    GELU,
+                )
+            h_codes = keep.tile([P, width], U32, name=f"h_codes{g}", align_bytes=64)
+            h_plane = keep.tile([P, width], U8, name=f"h_plane{g}", align_bytes=64)
+            nc.vector.quantize_mx(out=h_codes[:].bitcast(FP8X4), scales=h_plane[:], in_=hidden[:])
+            last = g == len(OUT_GROUPS) - 1
+            banks = []
+            for half in range(2):
+                if half == 0 or last:
+                    acc = psum_o.tile([P, 2, width], F32, name="acc")
+                banks.append(acc)
+                nc.tensor.matmul_mx(
+                    out=acc[:, half, :],
+                    lhsT=w2_codes[:, half * P : (half + 1) * P].bitcast(FP8X4),
+                    lhsT_scale=w2_plane[:, half * P : (half + 1) * P],
+                    rhs=h_codes[:].bitcast(FP8X4),
+                    rhs_scale=h_plane[:],
+                    start=True,
+                    stop=True,
+                )
+            if last:
+                low = keep.tile([P, width], F32, name="result_low")
+                high = keep.tile([P, width], F32, name="result_high")
+                nc.scalar.copy(low[:], banks[0][:, 0, :])
+                nc.scalar.dma_start(out[0:P, start : start + width], low[:])
+                nc.vector.tensor_copy(high[:], banks[1][:, 1, :])
+                nc.sync.dma_start(out[P : 2 * P, start : start + width], high[:])
+            else:
+                result = keep.tile([P, 2, width], F32, name=f"result{g}")
+                if g >= len(OUT_GROUPS) - 1 - 1:
+                    nc.scalar.copy(result[:], acc[:])
+                else:
+                    nc.vector.tensor_copy(result[:], acc[:])
+                nc.sync.dma_start(out_rows[:, :, start : start + width], result[:])
+            start = start + width

@@ -17,8 +17,10 @@ GELU = mybir.ActivationFunctionType.Gelu_apprx_tanh
 P = 128
 PACK = 4
 BLOCK = 128
+BLOCKS = S // BLOCK
 WORD_GATHERS = (256, 256, 512)
-OUT_GROUPS = (128,) * 8
+SCALAR_SHARE = 40
+COPY_LAG = 0
 
 
 def tile_picked_phmlp_gelu_p_kernel(tc, x_words, x_scales, w1, w2_words, w2_scales, offs, out):
@@ -31,49 +33,44 @@ def tile_picked_phmlp_gelu_p_kernel(tc, x_words, x_scales, w1, w2_words, w2_scal
         offsets = keep.tile([P, S // 16], U16, name="offsets")
         nc.sync.dma_start(offsets[:], offs)
 
-        scale_window = keep.tile([P, T], U8, name="scale_window", align_bytes=64)
-        nc.sync.dma_start(scale_window[:].bitcast(I32), x_scales[0].bitcast(I32).unsqueeze(1).to_broadcast([16, 8, T // 4]))
+        w1_raw = keep.tile([P, PACK, H], F32, name="w1_raw", tag="w1_raw_then_w2_plane", align_bytes=64)
+        nc.scalar.dma_start(w1_raw[:], w1.rearrange("(p j) c -> p j c", j=PACK))
+        word_window = keep.tile([P, T], U32, name="word_window", align_bytes=64)
+        nc.scalar.dma_start(word_window[:].bitcast(I32), x_words[0].rearrange("p n t -> p (n t)").bitcast(I32))
+        w2_codes = keep.tile([P, N], U32, name="w2_codes", align_bytes=64)
+        nc.scalar.dma_start(w2_codes[:].bitcast(I32), w2_words[0].rearrange("p n t -> p (n t)").bitcast(I32))
 
-        x_plane = keep.tile([P, S], U8, name="x_plane", align_bytes=64)
-        nc.vector.memset(x_plane[:].bitcast(I32), 0)
+        scale_window = keep.tile([P, T], U8, name="scale_window", tag="vector_steps", align_bytes=64)
+        nc.vector.memset(scale_window[:].bitcast(I32), 0)
+        nc.sync.dma_start(scale_window[0:P:8, :].bitcast(I32), x_scales[0].bitcast(I32))
+
         warm = keep.tile([P, 8], F32, name="warm")
         nc.vector.memset(warm[:, 0:1], 0.0)
         nc.scalar.activation(warm[:, 4:5], warm[:, 0:1], GELU)
 
-        w1_rows = w1.rearrange("(p j) c -> p j c", j=PACK)
-        w1_raw = []
-        for half in range(2):
-            raw = keep.tile([P, PACK, H // 2], F32, name=f"w1_raw{half}")
-            nc.sync.dma_start(raw[:], w1_rows[:, :, half * (H // 2) : (half + 1) * (H // 2)])
-            w1_raw.append(raw)
-
-        w2_plane = keep.tile([P, N], U8, name="w2_plane", align_bytes=64)
-        for q in range(4):
-            nc.sync.dma_start(
-                w2_plane[32 * q : 32 * q + 32, :].bitcast(I32),
-                w2_scales[0, 4 * q : 4 * q + 4, :].bitcast(I32).unsqueeze(0).to_broadcast([8, 4, N // 4]),
-            )
-
-        word_window = keep.tile([P, T], U32, name="word_window", align_bytes=64)
-        nc.sync.dma_start(word_window[:].bitcast(I32), x_words[0].rearrange("p n t -> p (n t)").bitcast(I32))
-
-        w2_codes = keep.tile([P, N], U32, name="w2_codes", align_bytes=64)
-        nc.sync.dma_start(w2_codes[:].bitcast(I32), w2_words[0].rearrange("p n t -> p (n t)").bitcast(I32))
+        x_plane = keep.tile([P, S], U8, name="x_plane", align_bytes=64)
+        nc.vector.memset(x_plane[:].bitcast(I32), 0)
 
         picked_scales = keep.tile([P, S], U8, name="picked_scales", align_bytes=64)
         nc.vector.tensor_copy(picked_scales[:], scale_window[:].indirect(offsets[:]))
         for q in range(4):
             nc.sync.dma_start(x_plane[32 * q : 32 * q + 4, :].bitcast(I32), picked_scales[32 * q : 32 * q + 32 : 8, :].bitcast(I32))
 
-        w1_grouped = keep.tile([P, H * PACK], BF16, name="w1_grouped", align_bytes=64)
+        w1_grouped = keep.tile([P, H * PACK], BF16, name="w1_grouped", tag="vector_steps", align_bytes=64)
         grouped_view = w1_grouped[:].rearrange("p (t m j) -> p m t j", t=PACK, j=PACK)
-        for half in range(2):
-            nc.scalar.copy(grouped_view[:, half * 64 : (half + 1) * 64], w1_raw[half][:].rearrange("p j (m t) -> p m t j", t=PACK))
+        raw_view = w1_raw[:].rearrange("p j (m t) -> p m t j", t=PACK)
+        nc.scalar.copy(grouped_view[:, 0:SCALAR_SHARE], raw_view[:, 0:SCALAR_SHARE])
+        nc.vector.tensor_copy(grouped_view[:, SCALAR_SHARE:P], raw_view[:, SCALAR_SHARE:P])
         w1_codes = keep.tile([P, H], U32, name="w1_codes", align_bytes=64)
         w1_plane = keep.tile([P, H], U8, name="w1_plane", align_bytes=64)
         nc.vector.quantize_mx(out=w1_codes[:].bitcast(FP8X4), scales=w1_plane[:], in_=w1_grouped[:])
 
-        picked_words = keep.tile([P, S], U32, name="picked_words", align_bytes=64)
+        w2_plane = keep.tile([P, N], U8, name="w2_plane", tag="w1_raw_then_w2_plane", align_bytes=64)
+        nc.gpsimd.memset(w2_plane[:].bitcast(I32), 0)
+        for q in range(4):
+            nc.sync.dma_start(w2_plane[32 * q : 32 * q + 4, :].bitcast(I32), w2_scales[0, 4 * q : 4 * q + 4, :].bitcast(I32))
+
+        picked_words = keep.tile([P, S], U32, name="picked_words", tag="vector_steps", align_bytes=64)
         start = 0
         for width in WORD_GATHERS:
             nc.vector.tensor_copy(
@@ -83,36 +80,30 @@ def tile_picked_phmlp_gelu_p_kernel(tc, x_words, x_scales, w1, w2_words, w2_scal
             start = start + width
 
         out_rows = out.rearrange("(h p) n -> p h n", p=P)
-        start = 0
-        for g, width in enumerate(OUT_GROUPS):
-            hidden = keep.tile([P, width * PACK], BF16, name=f"hidden{g}", align_bytes=64)
-            for b in range(width // BLOCK):
-                cols = slice(start + b * BLOCK, start + (b + 1) * BLOCK)
-                pre = psum_h.tile([P, PACK, BLOCK], F32, name="pre")
-                for t in range(PACK):
-                    nc.tensor.matmul_mx(
-                        out=pre[:, t, :],
-                        lhsT=w1_codes[:, t * P : (t + 1) * P].bitcast(FP8X4),
-                        lhsT_scale=w1_plane[:, t * P : (t + 1) * P],
-                        rhs=picked_words[:, cols].bitcast(FP8X4),
-                        rhs_scale=x_plane[:, cols],
-                        start=True,
-                        stop=True,
-                    )
-                nc.scalar.activation(
-                    hidden[:, b * BLOCK * PACK : (b + 1) * BLOCK * PACK].rearrange("p (n t) -> p n t", t=PACK),
-                    pre[:].rearrange("p t n -> p n t"),
-                    GELU,
+        banks = {}
+
+        def multiply(b):
+            cols = slice(b * BLOCK, (b + 1) * BLOCK)
+            pre = psum_h.tile([P, PACK, BLOCK], F32, name="pre")
+            for t in range(PACK):
+                nc.tensor.matmul_mx(
+                    out=pre[:, t, :],
+                    lhsT=w1_codes[:, t * P : (t + 1) * P].bitcast(FP8X4),
+                    lhsT_scale=w1_plane[:, t * P : (t + 1) * P],
+                    rhs=picked_words[:, cols].bitcast(FP8X4),
+                    rhs_scale=x_plane[:, cols],
+                    start=True,
+                    stop=True,
                 )
-            h_codes = keep.tile([P, width], U32, name=f"h_codes{g}", align_bytes=64)
-            h_plane = keep.tile([P, width], U8, name=f"h_plane{g}", align_bytes=64)
+            hidden = keep.tile([P, BLOCK * PACK], BF16, name=f"hidden{b}", align_bytes=64)
+            nc.scalar.activation(hidden[:].rearrange("p (n t) -> p n t", t=PACK), pre[:].rearrange("p t n -> p n t"), GELU)
+            h_codes = keep.tile([P, BLOCK], U32, name=f"h_codes{b}", align_bytes=64)
+            h_plane = keep.tile([P, BLOCK], U8, name=f"h_plane{b}", align_bytes=64)
             nc.vector.quantize_mx(out=h_codes[:].bitcast(FP8X4), scales=h_plane[:], in_=hidden[:])
-            last = g == len(OUT_GROUPS) - 1
-            banks = []
             for half in range(2):
-                if half == 0 or last:
-                    acc = psum_o.tile([P, 2, width], F32, name="acc")
-                banks.append(acc)
+                if half == 0 or b == BLOCKS - 1:
+                    acc = psum_o.tile([P, 2, BLOCK], F32, name="acc")
+                banks[b, half] = acc
                 nc.tensor.matmul_mx(
                     out=acc[:, half, :],
                     lhsT=w2_codes[:, half * P : (half + 1) * P].bitcast(FP8X4),
@@ -122,18 +113,24 @@ def tile_picked_phmlp_gelu_p_kernel(tc, x_words, x_scales, w1, w2_words, w2_scal
                     start=True,
                     stop=True,
                 )
-            if last:
-                low = keep.tile([P, width], F32, name="result_low")
-                high = keep.tile([P, width], F32, name="result_high")
-                nc.scalar.copy(low[:], banks[0][:, 0, :])
-                nc.scalar.dma_start(out[0:P, start : start + width], low[:])
-                nc.vector.tensor_copy(high[:], banks[1][:, 1, :])
-                nc.sync.dma_start(out[P : 2 * P, start : start + width], high[:])
+
+        def store(b):
+            cols = slice(b * BLOCK, (b + 1) * BLOCK)
+            result = keep.tile([P, 2, BLOCK], F32, name=f"result{b}", align_bytes=64)
+            if b == BLOCKS - 1:
+                nc.scalar.copy(result[:, 0, :], banks[b, 0][:, 0, :])
+                nc.scalar.dma_start(out[0:P, cols], result[:, 0, :])
+                nc.vector.tensor_copy(result[:, 1, :], banks[b, 1][:, 1, :])
+                nc.sync.dma_start(out[P : 2 * P, cols], result[:, 1, :])
+                return
+            if b == BLOCKS - 2:
+                nc.scalar.copy(result[:], banks[b, 0][:])
             else:
-                result = keep.tile([P, 2, width], F32, name=f"result{g}")
-                if g >= len(OUT_GROUPS) - 1 - 1:
-                    nc.scalar.copy(result[:], acc[:])
-                else:
-                    nc.vector.tensor_copy(result[:], acc[:])
-                nc.sync.dma_start(out_rows[:, :, start : start + width], result[:])
-            start = start + width
+                nc.vector.tensor_copy(result[:], banks[b, 0][:])
+            nc.sync.dma_start(out_rows[:, :, cols], result[:])
+
+        for b in range(BLOCKS + COPY_LAG):
+            if b < BLOCKS:
+                multiply(b)
+            if b >= COPY_LAG:
+                store(b - COPY_LAG)

@@ -33,21 +33,28 @@ def tile_picked_phmlp_gelu_p_kernel(tc, x_words, x_scales, w1, w2_words, w2_scal
         offsets = keep.tile([P, S // 16], U16, name="offsets")
         nc.sync.dma_start(offsets[:], offs)
 
-        w1_raw = keep.tile([P, PACK, H], F32, name="w1_raw", tag="w1_raw_then_w2_plane", align_bytes=64)
-        nc.scalar.dma_start(w1_raw[:], w1.rearrange("(p j) c -> p j c", j=PACK))
-        word_window = keep.tile([P, T], U32, name="word_window", align_bytes=64)
-        nc.scalar.dma_start(word_window[:].bitcast(I32), x_words[0].rearrange("p n t -> p (n t)").bitcast(I32))
-        w2_codes = keep.tile([P, N], U32, name="w2_codes", align_bytes=64)
-        nc.scalar.dma_start(w2_codes[:].bitcast(I32), w2_words[0].rearrange("p n t -> p (n t)").bitcast(I32))
-
-        scale_window = keep.tile([P, T], U8, name="scale_window", tag="vector_steps", align_bytes=64)
-        nc.vector.memset(scale_window[:].bitcast(I32), 0)
+        scale_window = keep.tile([P, T], U8, name="scale_window", align_bytes=64)
+        nc.vector.memset(scale_window[:, 0:1280].bitcast(I32), 0)
+        nc.gpsimd.memset(scale_window[:, 1280:T].bitcast(I32), 0)
         nc.sync.dma_start(scale_window[0:P:8, :].bitcast(I32), x_scales[0].bitcast(I32))
+
+        w2_codes = keep.tile([P, N], U32, name="w2_codes", align_bytes=64)
+        nc.sync.dma_start(w2_codes[:].bitcast(I32), w2_words[0].rearrange("p n t -> p (n t)").bitcast(I32))
+
+        w1_raw = keep.tile([P, PACK, H], F32, name="w1_raw")
+        nc.sync.dma_start(w1_raw[:], w1.rearrange("(p j) c -> p j c", j=PACK))
+
+        w2_plane = keep.tile([P, N], U8, name="w2_plane", align_bytes=64)
+        nc.vector.memset(w2_plane[:].bitcast(I32), 0)
+        word_window = keep.tile([P, T], U32, name="word_window", align_bytes=64)
+        for q in range(4):
+            if q == 3:
+                nc.sync.dma_start(word_window[:].bitcast(I32), x_words[0].rearrange("p n t -> p (n t)").bitcast(I32))
+            nc.sync.dma_start(w2_plane[32 * q : 32 * q + 4, :].bitcast(I32), w2_scales[0, 4 * q : 4 * q + 4, :].bitcast(I32))
 
         warm = keep.tile([P, 8], F32, name="warm")
         nc.vector.memset(warm[:, 0:1], 0.0)
         nc.scalar.activation(warm[:, 4:5], warm[:, 0:1], GELU)
-
         x_plane = keep.tile([P, S], U8, name="x_plane", align_bytes=64)
         nc.vector.memset(x_plane[:].bitcast(I32), 0)
 
@@ -56,7 +63,7 @@ def tile_picked_phmlp_gelu_p_kernel(tc, x_words, x_scales, w1, w2_words, w2_scal
         for q in range(4):
             nc.sync.dma_start(x_plane[32 * q : 32 * q + 4, :].bitcast(I32), picked_scales[32 * q : 32 * q + 32 : 8, :].bitcast(I32))
 
-        w1_grouped = keep.tile([P, H * PACK], BF16, name="w1_grouped", tag="vector_steps", align_bytes=64)
+        w1_grouped = keep.tile([P, H * PACK], BF16, name="w1_grouped", align_bytes=64)
         grouped_view = w1_grouped[:].rearrange("p (t m j) -> p m t j", t=PACK, j=PACK)
         raw_view = w1_raw[:].rearrange("p j (m t) -> p m t j", t=PACK)
         nc.scalar.copy(grouped_view[:, 0:SCALAR_SHARE], raw_view[:, 0:SCALAR_SHARE])
@@ -65,12 +72,7 @@ def tile_picked_phmlp_gelu_p_kernel(tc, x_words, x_scales, w1, w2_words, w2_scal
         w1_plane = keep.tile([P, H], U8, name="w1_plane", align_bytes=64)
         nc.vector.quantize_mx(out=w1_codes[:].bitcast(FP8X4), scales=w1_plane[:], in_=w1_grouped[:])
 
-        w2_plane = keep.tile([P, N], U8, name="w2_plane", tag="w1_raw_then_w2_plane", align_bytes=64)
-        nc.gpsimd.memset(w2_plane[:].bitcast(I32), 0)
-        for q in range(4):
-            nc.sync.dma_start(w2_plane[32 * q : 32 * q + 4, :].bitcast(I32), w2_scales[0, 4 * q : 4 * q + 4, :].bitcast(I32))
-
-        picked_words = keep.tile([P, S], U32, name="picked_words", tag="vector_steps", align_bytes=64)
+        picked_words = keep.tile([P, S], U32, name="picked_words", align_bytes=64)
         start = 0
         for width in WORD_GATHERS:
             nc.vector.tensor_copy(

@@ -19,7 +19,7 @@ PACK = 4
 BLOCK = 128
 BLOCKS = S // BLOCK
 WORD_GATHERS = (256, 256, 512)
-SCALAR_SHARE = 40
+SCALAR_SHARE = 56
 COPY_LAG = 0
 
 
@@ -34,8 +34,7 @@ def tile_picked_phmlp_gelu_p_kernel(tc, x_words, x_scales, w1, w2_words, w2_scal
         nc.sync.dma_start(offsets[:], offs)
 
         scale_window = keep.tile([P, T], U8, name="scale_window", align_bytes=64)
-        nc.vector.memset(scale_window[:, 0:1280].bitcast(I32), 0)
-        nc.gpsimd.memset(scale_window[:, 1280:T].bitcast(I32), 0)
+        nc.vector.memset(scale_window[:].bitcast(I32), 0)
         nc.sync.dma_start(scale_window[0:P:8, :].bitcast(I32), x_scales[0].bitcast(I32))
 
         w2_codes = keep.tile([P, N], U32, name="w2_codes", align_bytes=64)
@@ -52,9 +51,6 @@ def tile_picked_phmlp_gelu_p_kernel(tc, x_words, x_scales, w1, w2_words, w2_scal
                 nc.sync.dma_start(word_window[:].bitcast(I32), x_words[0].rearrange("p n t -> p (n t)").bitcast(I32))
             nc.sync.dma_start(w2_plane[32 * q : 32 * q + 4, :].bitcast(I32), w2_scales[0, 4 * q : 4 * q + 4, :].bitcast(I32))
 
-        warm = keep.tile([P, 8], F32, name="warm")
-        nc.vector.memset(warm[:, 0:1], 0.0)
-        nc.scalar.activation(warm[:, 4:5], warm[:, 0:1], GELU)
         x_plane = keep.tile([P, S], U8, name="x_plane", align_bytes=64)
         nc.vector.memset(x_plane[:].bitcast(I32), 0)
 
@@ -70,7 +66,23 @@ def tile_picked_phmlp_gelu_p_kernel(tc, x_words, x_scales, w1, w2_words, w2_scal
         nc.vector.tensor_copy(grouped_view[:, SCALAR_SHARE:P], raw_view[:, SCALAR_SHARE:P])
         w1_codes = keep.tile([P, H], U32, name="w1_codes", align_bytes=64)
         w1_plane = keep.tile([P, H], U8, name="w1_plane", align_bytes=64)
-        nc.vector.quantize_mx(out=w1_codes[:].bitcast(FP8X4), scales=w1_plane[:], in_=w1_grouped[:])
+        for t in range(PACK):
+            nc.vector.quantize_mx(
+                out=w1_codes[:, t * P : (t + 1) * P].bitcast(FP8X4),
+                scales=w1_plane[:, t * P : (t + 1) * P],
+                in_=w1_grouped[:, t * P * PACK : (t + 1) * P * PACK],
+            )
+        heat = psum_o.tile([P, 2, BLOCK], F32, name="acc")
+        for repeat in range(9):
+            nc.tensor.matmul_mx(
+                out=heat[:, 0, :],
+                lhsT=w1_codes[:, 0:P].bitcast(FP8X4),
+                lhsT_scale=w1_plane[:, 0:P],
+                rhs=w1_codes[:, 0:P].bitcast(FP8X4),
+                rhs_scale=w1_plane[:, 0:P],
+                start=True,
+                stop=True,
+            )
 
         picked_words = keep.tile([P, S], U32, name="picked_words", align_bytes=64)
         start = 0

@@ -19,7 +19,8 @@ PACK = 4
 BLOCK = 128
 BLOCKS = S // BLOCK
 WORD_GATHERS = (256, 256, 512)
-SCALAR_SHARE = 56
+SCALAR_SHARE = 72
+LEAD = 256
 COPY_LAG = 0
 
 
@@ -33,15 +34,15 @@ def tile_picked_phmlp_gelu_p_kernel(tc, x_words, x_scales, w1, w2_words, w2_scal
         offsets = keep.tile([P, S // 16], U16, name="offsets")
         nc.sync.dma_start(offsets[:], offs)
 
-        scale_window = keep.tile([P, T], U8, name="scale_window", align_bytes=64)
+        w1_raw = keep.tile([P, PACK * H], F32, name="w1_raw")
+        w1_rows = w1.rearrange("(p j) c -> p (j c)", j=PACK)
+        nc.sync.dma_start(w1_raw[:, 0:LEAD], w1_rows[:, 0:LEAD])
+
+        scale_window = keep.tile([P, T], U8, name="scale_window", tag="window", align_bytes=64)
         nc.vector.memset(scale_window[:].bitcast(I32), 0)
         nc.sync.dma_start(scale_window[0:P:8, :].bitcast(I32), x_scales[0].bitcast(I32))
 
-        w2_codes = keep.tile([P, N], U32, name="w2_codes", align_bytes=64)
-        nc.sync.dma_start(w2_codes[:].bitcast(I32), w2_words[0].rearrange("p n t -> p (n t)").bitcast(I32))
-
-        w1_raw = keep.tile([P, PACK, H], F32, name="w1_raw")
-        nc.sync.dma_start(w1_raw[:], w1.rearrange("(p j) c -> p j c", j=PACK))
+        nc.sync.dma_start(w1_raw[:, LEAD : PACK * H], w1_rows[:, LEAD : PACK * H])
 
         w2_plane = keep.tile([P, N], U8, name="w2_plane", align_bytes=64)
         nc.vector.memset(w2_plane[:].bitcast(I32), 0)
@@ -51,6 +52,10 @@ def tile_picked_phmlp_gelu_p_kernel(tc, x_words, x_scales, w1, w2_words, w2_scal
                 nc.sync.dma_start(word_window[:].bitcast(I32), x_words[0].rearrange("p n t -> p (n t)").bitcast(I32))
             nc.sync.dma_start(w2_plane[32 * q : 32 * q + 4, :].bitcast(I32), w2_scales[0, 4 * q : 4 * q + 4, :].bitcast(I32))
 
+        warm = keep.tile([P, 2], F32, name="warm")
+        nc.vector.memset(warm[:, 0:1], 0.0)
+        nc.scalar.activation(warm[:, 1:2], warm[:, 0:1], GELU)
+
         x_plane = keep.tile([P, S], U8, name="x_plane", align_bytes=64)
         nc.vector.memset(x_plane[:].bitcast(I32), 0)
 
@@ -59,9 +64,12 @@ def tile_picked_phmlp_gelu_p_kernel(tc, x_words, x_scales, w1, w2_words, w2_scal
         for q in range(4):
             nc.sync.dma_start(x_plane[32 * q : 32 * q + 4, :].bitcast(I32), picked_scales[32 * q : 32 * q + 32 : 8, :].bitcast(I32))
 
-        w1_grouped = keep.tile([P, H * PACK], BF16, name="w1_grouped", align_bytes=64)
+        w2_codes = keep.tile([P, N], U32, name="w2_codes", tag="window", align_bytes=64)
+        nc.sync.dma_start(w2_codes[:].bitcast(I32), w2_words[0].rearrange("p n t -> p (n t)").bitcast(I32))
+
+        w1_grouped = keep.tile([P, H * PACK], BF16, name="w1_grouped", tag="staging", align_bytes=64)
         grouped_view = w1_grouped[:].rearrange("p (t m j) -> p m t j", t=PACK, j=PACK)
-        raw_view = w1_raw[:].rearrange("p j (m t) -> p m t j", t=PACK)
+        raw_view = w1_raw[:].rearrange("p (j m t) -> p m t j", j=PACK, t=PACK)
         nc.scalar.copy(grouped_view[:, 0:SCALAR_SHARE], raw_view[:, 0:SCALAR_SHARE])
         nc.vector.tensor_copy(grouped_view[:, SCALAR_SHARE:P], raw_view[:, SCALAR_SHARE:P])
         w1_codes = keep.tile([P, H], U32, name="w1_codes", align_bytes=64)
@@ -72,19 +80,8 @@ def tile_picked_phmlp_gelu_p_kernel(tc, x_words, x_scales, w1, w2_words, w2_scal
                 scales=w1_plane[:, t * P : (t + 1) * P],
                 in_=w1_grouped[:, t * P * PACK : (t + 1) * P * PACK],
             )
-        heat = psum_o.tile([P, 2, BLOCK], F32, name="acc")
-        for repeat in range(9):
-            nc.tensor.matmul_mx(
-                out=heat[:, 0, :],
-                lhsT=w1_codes[:, 0:P].bitcast(FP8X4),
-                lhsT_scale=w1_plane[:, 0:P],
-                rhs=w1_codes[:, 0:P].bitcast(FP8X4),
-                rhs_scale=w1_plane[:, 0:P],
-                start=True,
-                stop=True,
-            )
 
-        picked_words = keep.tile([P, S], U32, name="picked_words", align_bytes=64)
+        picked_words = keep.tile([P, S], U32, name="picked_words", tag="staging", align_bytes=64)
         start = 0
         for width in WORD_GATHERS:
             nc.vector.tensor_copy(

@@ -19,7 +19,7 @@ PACK = 4
 BLOCK = 128
 BLOCKS = S // BLOCK
 WORD_GATHERS = (256, 256, 512)
-SCALAR_SHARE = 72
+SCALAR_SHARE = 56
 LEAD = 256
 COPY_LAG = 0
 
@@ -67,7 +67,7 @@ def tile_picked_phmlp_gelu_p_kernel(tc, x_words, x_scales, w1, w2_words, w2_scal
         w2_codes = keep.tile([P, N], U32, name="w2_codes", tag="window", align_bytes=64)
         nc.sync.dma_start(w2_codes[:].bitcast(I32), w2_words[0].rearrange("p n t -> p (n t)").bitcast(I32))
 
-        w1_grouped = keep.tile([P, H * PACK], BF16, name="w1_grouped", tag="staging", align_bytes=64)
+        w1_grouped = keep.tile([P, H * PACK], BF16, name="w1_grouped", align_bytes=64)
         grouped_view = w1_grouped[:].rearrange("p (t m j) -> p m t j", t=PACK, j=PACK)
         raw_view = w1_raw[:].rearrange("p (j m t) -> p m t j", j=PACK, t=PACK)
         nc.scalar.copy(grouped_view[:, 0:SCALAR_SHARE], raw_view[:, 0:SCALAR_SHARE])
@@ -81,7 +81,7 @@ def tile_picked_phmlp_gelu_p_kernel(tc, x_words, x_scales, w1, w2_words, w2_scal
                 in_=w1_grouped[:, t * P * PACK : (t + 1) * P * PACK],
             )
 
-        picked_words = keep.tile([P, S], U32, name="picked_words", tag="staging", align_bytes=64)
+        picked_words = keep.tile([P, S], U32, name="picked_words", align_bytes=64)
         start = 0
         for width in WORD_GATHERS:
             nc.vector.tensor_copy(

@@ -19,7 +19,8 @@ PACK = 4
 BLOCK = 128
 BLOCKS = S // BLOCK
 WORD_GATHERS = (256, 256, 512)
-SCALAR_SHARE = 56
+SCALAR_SHARE = 24
+EARLY = 768
 LEAD = 256
 COPY_LAG = 0
 
@@ -38,7 +39,7 @@ def tile_picked_phmlp_gelu_p_kernel(tc, x_words, x_scales, w1, w2_words, w2_scal
         w1_rows = w1.rearrange("(p j) c -> p (j c)", j=PACK)
         nc.sync.dma_start(w1_raw[:, 0:LEAD], w1_rows[:, 0:LEAD])
 
-        scale_window = keep.tile([P, T], U8, name="scale_window", tag="window", align_bytes=64)
+        scale_window = keep.tile([P, T], U8, name="scale_window", align_bytes=64)
         nc.vector.memset(scale_window[:].bitcast(I32), 0)
         nc.sync.dma_start(scale_window[0:P:8, :].bitcast(I32), x_scales[0].bitcast(I32))
 
@@ -52,6 +53,9 @@ def tile_picked_phmlp_gelu_p_kernel(tc, x_words, x_scales, w1, w2_words, w2_scal
                 nc.sync.dma_start(word_window[:].bitcast(I32), x_words[0].rearrange("p n t -> p (n t)").bitcast(I32))
             nc.sync.dma_start(w2_plane[32 * q : 32 * q + 4, :].bitcast(I32), w2_scales[0, 4 * q : 4 * q + 4, :].bitcast(I32))
 
+        w2_codes = keep.tile([P, N], U32, name="w2_codes", align_bytes=64)
+        nc.sync.dma_start(w2_codes[:].bitcast(I32), w2_words[0].rearrange("p n t -> p (n t)").bitcast(I32))
+
         warm = keep.tile([P, 2], F32, name="warm")
         nc.vector.memset(warm[:, 0:1], 0.0)
         nc.scalar.activation(warm[:, 1:2], warm[:, 0:1], GELU)
@@ -60,18 +64,22 @@ def tile_picked_phmlp_gelu_p_kernel(tc, x_words, x_scales, w1, w2_words, w2_scal
         nc.vector.memset(x_plane[:].bitcast(I32), 0)
 
         picked_scales = keep.tile([P, S], U8, name="picked_scales", align_bytes=64)
-        nc.vector.tensor_copy(picked_scales[:], scale_window[:].indirect(offsets[:]))
-        for q in range(4):
-            nc.sync.dma_start(x_plane[32 * q : 32 * q + 4, :].bitcast(I32), picked_scales[32 * q : 32 * q + 32 : 8, :].bitcast(I32))
 
-        w2_codes = keep.tile([P, N], U32, name="w2_codes", tag="window", align_bytes=64)
-        nc.sync.dma_start(w2_codes[:].bitcast(I32), w2_words[0].rearrange("p n t -> p (n t)").bitcast(I32))
+        def move_scales(first, last):
+            for q in range(4):
+                nc.sync.dma_start(x_plane[32 * q : 32 * q + 4, first:last].bitcast(I32), picked_scales[32 * q : 32 * q + 32 : 8, first:last].bitcast(I32))
+
+        nc.vector.tensor_copy(picked_scales[:, 0:EARLY], scale_window[:].indirect(offsets[:, 0 : EARLY // 16]))
+        move_scales(0, EARLY)
+        nc.vector.tensor_copy(picked_scales[:, EARLY:S], scale_window[:].indirect(offsets[:, EARLY // 16 : S // 16]))
+        move_scales(EARLY, S)
 
         w1_grouped = keep.tile([P, H * PACK], BF16, name="w1_grouped", align_bytes=64)
-        grouped_view = w1_grouped[:].rearrange("p (t m j) -> p m t j", t=PACK, j=PACK)
-        raw_view = w1_raw[:].rearrange("p (j m t) -> p m t j", j=PACK, t=PACK)
-        nc.scalar.copy(grouped_view[:, 0:SCALAR_SHARE], raw_view[:, 0:SCALAR_SHARE])
-        nc.vector.tensor_copy(grouped_view[:, SCALAR_SHARE:P], raw_view[:, SCALAR_SHARE:P])
+        grouped_view = w1_grouped[:].rearrange("p (u e m j) -> p u m j e", u=2, e=2, j=PACK)
+        raw_view = w1_raw[:].rearrange("p (j m u e) -> p u m j e", j=PACK, u=2, e=2)
+        nc.scalar.copy(grouped_view[:, 0, 0:SCALAR_SHARE], raw_view[:, 0, 0:SCALAR_SHARE])
+        nc.vector.tensor_copy(grouped_view[:, 0, SCALAR_SHARE:P], raw_view[:, 0, SCALAR_SHARE:P])
+        nc.scalar.copy(grouped_view[:, 1], raw_view[:, 1])
         w1_codes = keep.tile([P, H], U32, name="w1_codes", align_bytes=64)
         w1_plane = keep.tile([P, H], U8, name="w1_plane", align_bytes=64)
         for t in range(PACK):
@@ -79,6 +87,18 @@ def tile_picked_phmlp_gelu_p_kernel(tc, x_words, x_scales, w1, w2_words, w2_scal
                 out=w1_codes[:, t * P : (t + 1) * P].bitcast(FP8X4),
                 scales=w1_plane[:, t * P : (t + 1) * P],
                 in_=w1_grouped[:, t * P * PACK : (t + 1) * P * PACK],
+            )
+
+        heat = psum_o.tile([P, 2 * BLOCK], F32, name="acc")
+        for repeat in range(4):
+            nc.tensor.matmul_mx(
+                out=heat[:],
+                lhsT=w1_codes[:, 0:P].bitcast(FP8X4),
+                lhsT_scale=w1_plane[:, 0:P],
+                rhs=w1_codes[:, 0 : 2 * P].bitcast(FP8X4),
+                rhs_scale=w1_plane[:, 0 : 2 * P],
+                start=True,
+                stop=True,
             )
 
         picked_words = keep.tile([P, S], U32, name="picked_words", align_bytes=64)

@@ -16,40 +16,47 @@ GELU = mybir.ActivationFunctionType.Gelu_apprx_tanh
 
 P = 128
 PACK = 4
-BLOCK = 128
-BLOCKS = S // BLOCK
-WORD_GATHERS = (256, 256, 512)
+QUADRANTS = 4
+LIST_ROWS = 16
+STEP = 128
+STEPS = S // STEP
+PAIRED_STEPS = STEPS - 2
+W1_LEAD = 256
 SCALAR_SHARE = 24
-EARLY = 768
-LEAD = 256
-COPY_LAG = 0
+EARLY_PLACES = 768
+WORD_GATHERS = (256, 256, 512)
+FIRST_BANKS, SECOND_BANKS = 5, 3
+TENSOR_WARM_UPS = 4
 
 
 def tile_picked_phmlp_gelu_p_kernel(tc, x_words, x_scales, w1, w2_words, w2_scales, offs, out):
     nc = tc.nc
     with ExitStack() as ctx:
         keep = ctx.enter_context(tc.tile_pool(name="keep", bufs=1))
-        psum_h = ctx.enter_context(tc.psum_pool(name="psum_h", bufs=4))
-        psum_o = ctx.enter_context(tc.psum_pool(name="psum_o", bufs=4))
+        psum_h = ctx.enter_context(tc.psum_pool(name="psum_h", bufs=FIRST_BANKS))
+        psum_o = ctx.enter_context(tc.psum_pool(name="psum_o", bufs=SECOND_BANKS))
 
-        offsets = keep.tile([P, S // 16], U16, name="offsets")
+        offsets = keep.tile([P, S // LIST_ROWS], U16, name="offsets")
         nc.sync.dma_start(offsets[:], offs)
+
+        def entries(first, last):
+            return offsets[:, first // LIST_ROWS : last // LIST_ROWS]
 
         w1_raw = keep.tile([P, PACK * H], F32, name="w1_raw")
         w1_rows = w1.rearrange("(p j) c -> p (j c)", j=PACK)
-        nc.sync.dma_start(w1_raw[:, 0:LEAD], w1_rows[:, 0:LEAD])
+        nc.sync.dma_start(w1_raw[:, 0:W1_LEAD], w1_rows[:, 0:W1_LEAD])
 
         scale_window = keep.tile([P, T], U8, name="scale_window", align_bytes=64)
         nc.vector.memset(scale_window[:].bitcast(I32), 0)
         nc.sync.dma_start(scale_window[0:P:8, :].bitcast(I32), x_scales[0].bitcast(I32))
 
-        nc.sync.dma_start(w1_raw[:, LEAD : PACK * H], w1_rows[:, LEAD : PACK * H])
+        nc.sync.dma_start(w1_raw[:, W1_LEAD : PACK * H], w1_rows[:, W1_LEAD : PACK * H])
 
         w2_plane = keep.tile([P, N], U8, name="w2_plane", align_bytes=64)
         nc.vector.memset(w2_plane[:].bitcast(I32), 0)
         word_window = keep.tile([P, T], U32, name="word_window", align_bytes=64)
-        for q in range(4):
-            if q == 3:
+        for q in range(QUADRANTS):
+            if q == QUADRANTS - 1:
                 nc.sync.dma_start(word_window[:].bitcast(I32), x_words[0].rearrange("p n t -> p (n t)").bitcast(I32))
             nc.sync.dma_start(w2_plane[32 * q : 32 * q + 4, :].bitcast(I32), w2_scales[0, 4 * q : 4 * q + 4, :].bitcast(I32))
 
@@ -62,17 +69,14 @@ def tile_picked_phmlp_gelu_p_kernel(tc, x_words, x_scales, w1, w2_words, w2_scal
 
         x_plane = keep.tile([P, S], U8, name="x_plane", align_bytes=64)
         nc.vector.memset(x_plane[:].bitcast(I32), 0)
-
         picked_scales = keep.tile([P, S], U8, name="picked_scales", align_bytes=64)
-
-        def move_scales(first, last):
-            for q in range(4):
-                nc.sync.dma_start(x_plane[32 * q : 32 * q + 4, first:last].bitcast(I32), picked_scales[32 * q : 32 * q + 32 : 8, first:last].bitcast(I32))
-
-        nc.vector.tensor_copy(picked_scales[:, 0:EARLY], scale_window[:].indirect(offsets[:, 0 : EARLY // 16]))
-        move_scales(0, EARLY)
-        nc.vector.tensor_copy(picked_scales[:, EARLY:S], scale_window[:].indirect(offsets[:, EARLY // 16 : S // 16]))
-        move_scales(EARLY, S)
+        for first, last in ((0, EARLY_PLACES), (EARLY_PLACES, S)):
+            nc.vector.tensor_copy(picked_scales[:, first:last], scale_window[:].indirect(entries(first, last)))
+            for q in range(QUADRANTS):
+                nc.sync.dma_start(
+                    x_plane[32 * q : 32 * q + 4, first:last].bitcast(I32),
+                    picked_scales[32 * q : 32 * q + 32 : 8, first:last].bitcast(I32),
+                )
 
         w1_grouped = keep.tile([P, H * PACK], BF16, name="w1_grouped", align_bytes=64)
         grouped_view = w1_grouped[:].rearrange("p (u e m j) -> p u m j e", u=2, e=2, j=PACK)
@@ -89,8 +93,8 @@ def tile_picked_phmlp_gelu_p_kernel(tc, x_words, x_scales, w1, w2_words, w2_scal
                 in_=w1_grouped[:, t * P * PACK : (t + 1) * P * PACK],
             )
 
-        heat = psum_o.tile([P, 2 * BLOCK], F32, name="acc")
-        for repeat in range(4):
+        heat = psum_o.tile([P, 2 * P], F32, name="acc")
+        for repeat in range(TENSOR_WARM_UPS):
             nc.tensor.matmul_mx(
                 out=heat[:],
                 lhsT=w1_codes[:, 0:P].bitcast(FP8X4),
@@ -102,20 +106,14 @@ def tile_picked_phmlp_gelu_p_kernel(tc, x_words, x_scales, w1, w2_words, w2_scal
             )
 
         picked_words = keep.tile([P, S], U32, name="picked_words", align_bytes=64)
-        start = 0
+        gathered = 0
         for width in WORD_GATHERS:
-            nc.vector.tensor_copy(
-                picked_words[:, start : start + width],
-                word_window[:].indirect(offsets[:, start // 16 : (start + width) // 16]),
-            )
-            start = start + width
+            nc.vector.tensor_copy(picked_words[:, gathered : gathered + width], word_window[:].indirect(entries(gathered, gathered + width)))
+            gathered = gathered + width
 
-        out_rows = out.rearrange("(h p) n -> p h n", p=P)
-        banks = {}
-
-        def multiply(b):
-            cols = slice(b * BLOCK, (b + 1) * BLOCK)
-            pre = psum_h.tile([P, PACK, BLOCK], F32, name="pre")
+        def hidden_codes(step):
+            cols = slice(step * STEP, (step + 1) * STEP)
+            pre = psum_h.tile([P, PACK, STEP], F32, name="pre")
             for t in range(PACK):
                 nc.tensor.matmul_mx(
                     out=pre[:, t, :],
@@ -126,42 +124,51 @@ def tile_picked_phmlp_gelu_p_kernel(tc, x_words, x_scales, w1, w2_words, w2_scal
                     start=True,
                     stop=True,
                 )
-            hidden = keep.tile([P, BLOCK * PACK], BF16, name=f"hidden{b}", align_bytes=64)
+            hidden = keep.tile([P, STEP * PACK], BF16, name=f"hidden{step}", align_bytes=64)
             nc.scalar.activation(hidden[:].rearrange("p (n t) -> p n t", t=PACK), pre[:].rearrange("p t n -> p n t"), GELU)
-            h_codes = keep.tile([P, BLOCK], U32, name=f"h_codes{b}", align_bytes=64)
-            h_plane = keep.tile([P, BLOCK], U8, name=f"h_plane{b}", align_bytes=64)
+            h_codes = keep.tile([P, STEP], U32, name=f"h_codes{step}", align_bytes=64)
+            h_plane = keep.tile([P, STEP], U8, name=f"h_plane{step}", align_bytes=64)
             nc.vector.quantize_mx(out=h_codes[:].bitcast(FP8X4), scales=h_plane[:], in_=hidden[:])
+            return h_codes, h_plane
+
+        def second_product(acc, half, h_codes, h_plane):
+            nc.tensor.matmul_mx(
+                out=acc[:, half, :],
+                lhsT=w2_codes[:, half * P : (half + 1) * P].bitcast(FP8X4),
+                lhsT_scale=w2_plane[:, half * P : (half + 1) * P],
+                rhs=h_codes[:].bitcast(FP8X4),
+                rhs_scale=h_plane[:],
+                start=True,
+                stop=True,
+            )
+
+        out_rows = out.rearrange("(h p) n -> p h n", p=P)
+        for step in range(STEPS - 1):
+            h_codes, h_plane = hidden_codes(step)
+            acc = psum_o.tile([P, 2, STEP], F32, name="acc")
             for half in range(2):
-                if half == 0 or b == BLOCKS - 1:
-                    acc = psum_o.tile([P, 2, BLOCK], F32, name="acc")
-                banks[b, half] = acc
-                nc.tensor.matmul_mx(
-                    out=acc[:, half, :],
-                    lhsT=w2_codes[:, half * P : (half + 1) * P].bitcast(FP8X4),
-                    lhsT_scale=w2_plane[:, half * P : (half + 1) * P],
-                    rhs=h_codes[:].bitcast(FP8X4),
-                    rhs_scale=h_plane[:],
-                    start=True,
-                    stop=True,
-                )
-
-        def store(b):
-            cols = slice(b * BLOCK, (b + 1) * BLOCK)
-            result = keep.tile([P, 2, BLOCK], F32, name=f"result{b}", align_bytes=64)
-            if b == BLOCKS - 1:
-                nc.scalar.copy(result[:, 0, :], banks[b, 0][:, 0, :])
-                nc.scalar.dma_start(out[0:P, cols], result[:, 0, :])
-                nc.vector.tensor_copy(result[:, 1, :], banks[b, 1][:, 1, :])
-                nc.sync.dma_start(out[P : 2 * P, cols], result[:, 1, :])
-                return
-            if b == BLOCKS - 2:
-                nc.scalar.copy(result[:], banks[b, 0][:])
+                second_product(acc, half, h_codes, h_plane)
+            if step < PAIRED_STEPS:
+                side = step % 2
+                if side == 0:
+                    pair = keep.tile([P, 2, 2 * STEP], F32, name=f"result{step}", align_bytes=64)
+                nc.vector.tensor_copy(pair[:, :, side * STEP : (side + 1) * STEP], acc[:])
+                if side == 1:
+                    nc.sync.dma_start(out_rows[:, :, (step - 1) * STEP : (step + 1) * STEP], pair[:])
             else:
-                nc.vector.tensor_copy(result[:], banks[b, 0][:])
-            nc.sync.dma_start(out_rows[:, :, cols], result[:])
+                result = keep.tile([P, 2, STEP], F32, name=f"result{step}", align_bytes=64)
+                nc.scalar.copy(result[:], acc[:])
+                nc.sync.dma_start(out_rows[:, :, step * STEP : (step + 1) * STEP], result[:])
 
-        for b in range(BLOCKS + COPY_LAG):
-            if b < BLOCKS:
-                multiply(b)
-            if b >= COPY_LAG:
-                store(b - COPY_LAG)
+        h_codes, h_plane = hidden_codes(STEPS - 1)
+        halves = []
+        for half in range(2):
+            acc = psum_o.tile([P, 2, STEP], F32, name="acc")
+            second_product(acc, half, h_codes, h_plane)
+            halves.append(acc)
+        cols = slice(S - STEP, S)
+        result = keep.tile([P, 2, STEP], F32, name=f"result{STEPS - 1}", align_bytes=64)
+        nc.scalar.copy(result[:, 0, :], halves[0][:, 0, :])
+        nc.scalar.dma_start(out[0:P, cols], result[:, 0, :])
+        nc.vector.tensor_copy(result[:, 1, :], halves[1][:, 1, :])
+        nc.sync.dma_start(out[P : 2 * P, cols], result[:, 1, :])

@@ -21,8 +21,9 @@ LIST_ROWS = 16
 STEP = 128
 STEPS = S // STEP
 PAIRED_STEPS = STEPS - 2
+STORE_GROUPS = ((0, 4), (4, 6))
 W1_LEAD = 256
-SCALAR_SHARE = 24
+SCALAR_SHARES = (64, 88)
 EARLY_PLACES = 768
 WORD_GATHERS = (256, 256, 512)
 FIRST_BANKS, SECOND_BANKS = 5, 3
@@ -44,13 +45,14 @@ def tile_picked_phmlp_gelu_p_kernel(tc, x_words, x_scales, w1, w2_words, w2_scal
 
         w1_raw = keep.tile([P, PACK * H], F32, name="w1_raw")
         w1_rows = w1.rearrange("(p j) c -> p (j c)", j=PACK)
-        nc.sync.dma_start(w1_raw[:, 0:W1_LEAD], w1_rows[:, 0:W1_LEAD])
+        nc.scalar.dma_start(w1_raw[:, 0:W1_LEAD], w1_rows[:, 0:W1_LEAD])
+        nc.sync.dma_start(w1_raw[:, W1_LEAD : 2 * W1_LEAD], w1_rows[:, W1_LEAD : 2 * W1_LEAD])
 
         scale_window = keep.tile([P, T], U8, name="scale_window", align_bytes=64)
         nc.vector.memset(scale_window[:].bitcast(I32), 0)
         nc.sync.dma_start(scale_window[0:P:8, :].bitcast(I32), x_scales[0].bitcast(I32))
 
-        nc.sync.dma_start(w1_raw[:, W1_LEAD : PACK * H], w1_rows[:, W1_LEAD : PACK * H])
+        nc.sync.dma_start(w1_raw[:, 2 * W1_LEAD : PACK * H], w1_rows[:, 2 * W1_LEAD : PACK * H])
 
         w2_plane = keep.tile([P, N], U8, name="w2_plane", align_bytes=64)
         nc.vector.memset(w2_plane[:].bitcast(I32), 0)
@@ -69,21 +71,23 @@ def tile_picked_phmlp_gelu_p_kernel(tc, x_words, x_scales, w1, w2_words, w2_scal
 
         x_plane = keep.tile([P, S], U8, name="x_plane", align_bytes=64)
         nc.vector.memset(x_plane[:].bitcast(I32), 0)
-        picked_scales = keep.tile([P, S], U8, name="picked_scales", align_bytes=64)
-        for first, last in ((0, EARLY_PLACES), (EARLY_PLACES, S)):
-            nc.vector.tensor_copy(picked_scales[:, first:last], scale_window[:].indirect(entries(first, last)))
+
+        def pick_scales(picked, first, last):
+            nc.vector.tensor_copy(picked[:], scale_window[:].indirect(entries(first, last)))
             for q in range(QUADRANTS):
-                nc.sync.dma_start(
-                    x_plane[32 * q : 32 * q + 4, first:last].bitcast(I32),
-                    picked_scales[32 * q : 32 * q + 32 : 8, first:last].bitcast(I32),
-                )
+                nc.sync.dma_start(x_plane[32 * q : 32 * q + 4, first:last].bitcast(I32), picked[32 * q : 32 * q + 32 : 8, :].bitcast(I32))
+
+        early_scales = keep.tile([P, EARLY_PLACES], U8, name="early_scales", align_bytes=64)
+        pick_scales(early_scales, 0, EARLY_PLACES)
+        late_scales = keep.tile([P, S - EARLY_PLACES], U8, name="late_scales", align_bytes=64)
+        pick_scales(late_scales, EARLY_PLACES, S)
 
         w1_grouped = keep.tile([P, H * PACK], BF16, name="w1_grouped", align_bytes=64)
         grouped_view = w1_grouped[:].rearrange("p (u e m j) -> p u m j e", u=2, e=2, j=PACK)
         raw_view = w1_raw[:].rearrange("p (j m u e) -> p u m j e", j=PACK, u=2, e=2)
-        nc.scalar.copy(grouped_view[:, 0, 0:SCALAR_SHARE], raw_view[:, 0, 0:SCALAR_SHARE])
-        nc.vector.tensor_copy(grouped_view[:, 0, SCALAR_SHARE:P], raw_view[:, 0, SCALAR_SHARE:P])
-        nc.scalar.copy(grouped_view[:, 1], raw_view[:, 1])
+        for u, share in enumerate(SCALAR_SHARES):
+            nc.scalar.copy(grouped_view[:, u, 0:share], raw_view[:, u, 0:share])
+            nc.vector.tensor_copy(grouped_view[:, u, share:P], raw_view[:, u, share:P])
         w1_codes = keep.tile([P, H], U32, name="w1_codes", align_bytes=64)
         w1_plane = keep.tile([P, H], U8, name="w1_plane", align_bytes=64)
         for t in range(PACK):
@@ -149,12 +153,13 @@ def tile_picked_phmlp_gelu_p_kernel(tc, x_words, x_scales, w1, w2_words, w2_scal
             for half in range(2):
                 second_product(acc, half, h_codes, h_plane)
             if step < PAIRED_STEPS:
-                side = step % 2
+                first, last = [g for g in STORE_GROUPS if g[0] <= step < g[1]][0]
+                side = step - first
                 if side == 0:
-                    pair = keep.tile([P, 2, 2 * STEP], F32, name=f"result{step}", align_bytes=64)
+                    pair = keep.tile([P, 2, (last - first) * STEP], F32, name=f"result{step}", align_bytes=64)
                 nc.vector.tensor_copy(pair[:, :, side * STEP : (side + 1) * STEP], acc[:])
-                if side == 1:
-                    nc.sync.dma_start(out_rows[:, :, (step - 1) * STEP : (step + 1) * STEP], pair[:])
+                if step == last - 1:
+                    nc.sync.dma_start(out_rows[:, :, first * STEP : last * STEP], pair[:])
             else:
                 result = keep.tile([P, 2, STEP], F32, name=f"result{step}", align_bytes=64)
                 nc.scalar.copy(result[:], acc[:])

@@ -174,6 +174,6 @@ def tile_picked_phmlp_gelu_p_kernel(tc, x_words, x_scales, w1, w2_words, w2_scal
         cols = slice(S - STEP, S)
         result = keep.tile([P, 2, STEP], F32, name=f"result{STEPS - 1}", align_bytes=64)
         nc.scalar.copy(result[:, 0, :], halves[0][:, 0, :])
-        nc.scalar.dma_start(out[0:P, cols], result[:, 0, :])
+        nc.sync.dma_start(out[0:P, cols], result[:, 0, :])
         nc.vector.tensor_copy(result[:, 1, :], halves[1][:, 1, :])
         nc.sync.dma_start(out[P : 2 * P, cols], result[:, 1, :])

@@ -20,8 +20,7 @@ QUADRANTS = 4
 LIST_ROWS = 16
 STEP = 128
 STEPS = S // STEP
-PAIRED_STEPS = STEPS - 2
-STORE_GROUPS = ((0, 4), (4, 6))
+STORE_GROUPS = ((0, 4), (4, STEPS - 2))
 W1_LEAD = 256
 SCALAR_SHARES = (64, 88)
 EARLY_PLACES = 768
@@ -38,14 +37,14 @@ def tile_picked_phmlp_gelu_p_kernel(tc, x_words, x_scales, w1, w2_words, w2_scal
         psum_o = ctx.enter_context(tc.psum_pool(name="psum_o", bufs=SECOND_BANKS))
 
         offsets = keep.tile([P, S // LIST_ROWS], U16, name="offsets")
-        nc.sync.dma_start(offsets[:], offs)
 
         def entries(first, last):
             return offsets[:, first // LIST_ROWS : last // LIST_ROWS]
 
         w1_raw = keep.tile([P, PACK * H], F32, name="w1_raw")
         w1_rows = w1.rearrange("(p j) c -> p (j c)", j=PACK)
-        nc.scalar.dma_start(w1_raw[:, 0:W1_LEAD], w1_rows[:, 0:W1_LEAD])
+        nc.sync.dma_start(w1_raw[:, 0:W1_LEAD], w1_rows[:, 0:W1_LEAD])
+        nc.sync.dma_start(offsets[:], offs)
         nc.sync.dma_start(w1_raw[:, W1_LEAD : 2 * W1_LEAD], w1_rows[:, W1_LEAD : 2 * W1_LEAD])
 
         scale_window = keep.tile([P, T], U8, name="scale_window", align_bytes=64)
@@ -75,7 +74,10 @@ def tile_picked_phmlp_gelu_p_kernel(tc, x_words, x_scales, w1, w2_words, w2_scal
         def pick_scales(picked, first, last):
             nc.vector.tensor_copy(picked[:], scale_window[:].indirect(entries(first, last)))
             for q in range(QUADRANTS):
-                nc.sync.dma_start(x_plane[32 * q : 32 * q + 4, first:last].bitcast(I32), picked[32 * q : 32 * q + 32 : 8, :].bitcast(I32))
+                nc.sync.dma_start(
+                    x_plane[32 * q : 32 * q + 4, first:last].bitcast(I32),
+                    picked[32 * q : 32 * q + 32 : 8, :].bitcast(I32),
+                )
 
         early_scales = keep.tile([P, EARLY_PLACES], U8, name="early_scales", align_bytes=64)
         pick_scales(early_scales, 0, EARLY_PLACES)
@@ -147,23 +149,26 @@ def tile_picked_phmlp_gelu_p_kernel(tc, x_words, x_scales, w1, w2_words, w2_scal
             )
 
         out_rows = out.rearrange("(h p) n -> p h n", p=P)
-        for step in range(STEPS - 1):
+
+        def step_result(step):
             h_codes, h_plane = hidden_codes(step)
             acc = psum_o.tile([P, 2, STEP], F32, name="acc")
             for half in range(2):
                 second_product(acc, half, h_codes, h_plane)
-            if step < PAIRED_STEPS:
-                first, last = [g for g in STORE_GROUPS if g[0] <= step < g[1]][0]
-                side = step - first
-                if side == 0:
-                    pair = keep.tile([P, 2, (last - first) * STEP], F32, name=f"result{step}", align_bytes=64)
-                nc.vector.tensor_copy(pair[:, :, side * STEP : (side + 1) * STEP], acc[:])
-                if step == last - 1:
-                    nc.sync.dma_start(out_rows[:, :, first * STEP : last * STEP], pair[:])
-            else:
-                result = keep.tile([P, 2, STEP], F32, name=f"result{step}", align_bytes=64)
-                nc.scalar.copy(result[:], acc[:])
-                nc.sync.dma_start(out_rows[:, :, step * STEP : (step + 1) * STEP], result[:])
+            return acc
+
+        for first, last in STORE_GROUPS:
+            for step in range(first, last):
+                acc = step_result(step)
+                if step == first:
+                    group = keep.tile([P, 2, (last - first) * STEP], F32, name=f"result{step}", align_bytes=64)
+                nc.vector.tensor_copy(group[:, :, (step - first) * STEP : (step - first + 1) * STEP], acc[:])
+            nc.sync.dma_start(out_rows[:, :, first * STEP : last * STEP], group[:])
+
+        acc = step_result(STEPS - 2)
+        result = keep.tile([P, 2, STEP], F32, name=f"result{STEPS - 2}", align_bytes=64)
+        nc.scalar.copy(result[:], acc[:])
+        nc.sync.dma_start(out_rows[:, :, S - 2 * STEP : S - STEP], result[:])
 
         h_codes, h_plane = hidden_codes(STEPS - 1)
         halves = []

@@ -21,8 +21,8 @@ LIST_ROWS = 16
 STEP = 128
 STEPS = S // STEP
 STORE_GROUPS = ((0, 4), (4, STEPS - 2))
-W1_LEAD = 256
-SCALAR_SHARES = (64, 88)
+HALF = H // 2
+SCALAR_SHARE = 32
 EARLY_PLACES = 768
 WORD_GATHERS = (256, 256, 512)
 FIRST_BANKS, SECOND_BANKS = 5, 3
@@ -41,17 +41,17 @@ def tile_picked_phmlp_gelu_p_kernel(tc, x_words, x_scales, w1, w2_words, w2_scal
         def entries(first, last):
             return offsets[:, first // LIST_ROWS : last // LIST_ROWS]
 
-        w1_raw = keep.tile([P, PACK * H], F32, name="w1_raw")
-        w1_rows = w1.rearrange("(p j) c -> p (j c)", j=PACK)
-        nc.sync.dma_start(w1_raw[:, 0:W1_LEAD], w1_rows[:, 0:W1_LEAD])
+        w1_rows = w1.rearrange("(p j) c -> p j c", j=PACK)
+        w1_raw = [keep.tile([P, PACK, HALF], F32, name=f"w1_raw{half}") for half in range(2)]
+        nc.sync.dma_start(w1_raw[0][:, 0:2, :], w1_rows[:, 0:2, 0:HALF])
         nc.sync.dma_start(offsets[:], offs)
-        nc.sync.dma_start(w1_raw[:, W1_LEAD : 2 * W1_LEAD], w1_rows[:, W1_LEAD : 2 * W1_LEAD])
 
         scale_window = keep.tile([P, T], U8, name="scale_window", align_bytes=64)
         nc.vector.memset(scale_window[:].bitcast(I32), 0)
         nc.sync.dma_start(scale_window[0:P:8, :].bitcast(I32), x_scales[0].bitcast(I32))
 
-        nc.sync.dma_start(w1_raw[:, 2 * W1_LEAD : PACK * H], w1_rows[:, 2 * W1_LEAD : PACK * H])
+        nc.sync.dma_start(w1_raw[0][:, 2:PACK, :], w1_rows[:, 2:PACK, 0:HALF])
+        nc.sync.dma_start(w1_raw[1][:], w1_rows[:, :, HALF:H])
 
         w2_plane = keep.tile([P, N], U8, name="w2_plane", align_bytes=64)
         nc.vector.memset(w2_plane[:].bitcast(I32), 0)
@@ -85,11 +85,16 @@ def tile_picked_phmlp_gelu_p_kernel(tc, x_words, x_scales, w1, w2_words, w2_scal
         pick_scales(late_scales, EARLY_PLACES, S)
 
         w1_grouped = keep.tile([P, H * PACK], BF16, name="w1_grouped", align_bytes=64)
+        groups = HALF // PACK
+        nc.scalar.copy(
+            w1_grouped[:].rearrange("p (t m j) -> p m j t", t=PACK, j=PACK)[:, 0:groups],
+            w1_raw[0][:].rearrange("p j (m t) -> p m j t", t=PACK),
+        )
         grouped_view = w1_grouped[:].rearrange("p (u e m j) -> p u m j e", u=2, e=2, j=PACK)
-        raw_view = w1_raw[:].rearrange("p (j m u e) -> p u m j e", j=PACK, u=2, e=2)
-        for u, share in enumerate(SCALAR_SHARES):
-            nc.scalar.copy(grouped_view[:, u, 0:share], raw_view[:, u, 0:share])
-            nc.vector.tensor_copy(grouped_view[:, u, share:P], raw_view[:, u, share:P])
+        raw_view = w1_raw[1][:].rearrange("p j (m u e) -> p u m j e", u=2, e=2)
+        nc.scalar.copy(grouped_view[:, 0, groups:P], raw_view[:, 0])
+        nc.scalar.copy(grouped_view[:, 1, groups : groups + SCALAR_SHARE], raw_view[:, 1, 0:SCALAR_SHARE])
+        nc.vector.tensor_copy(grouped_view[:, 1, groups + SCALAR_SHARE : P], raw_view[:, 1, SCALAR_SHARE:groups])
         w1_codes = keep.tile([P, H], U32, name="w1_codes", align_bytes=64)
         w1_plane = keep.tile([P, H], U8, name="w1_plane", align_bytes=64)
         for t in range(PACK):

@@ -20,7 +20,7 @@ QUADRANTS = 4
 LIST_ROWS = 16
 STEP = 128
 STEPS = S // STEP
-STORE_GROUPS = ((0, 4), (4, STEPS - 2))
+STORE_GROUPS = ((0, 3), (3, STEPS - 3))
 HALF = H // 2
 SCALAR_SHARE = 32
 EARLY_PLACES = 768
@@ -122,7 +122,7 @@ def tile_picked_phmlp_gelu_p_kernel(tc, x_words, x_scales, w1, w2_words, w2_scal
             nc.vector.tensor_copy(picked_words[:, gathered : gathered + width], word_window[:].indirect(entries(gathered, gathered + width)))
             gathered = gathered + width
 
-        def hidden_codes(step):
+        def first_product(step):
             cols = slice(step * STEP, (step + 1) * STEP)
             pre = psum_h.tile([P, PACK, STEP], F32, name="pre")
             for t in range(PACK):
@@ -135,10 +135,14 @@ def tile_picked_phmlp_gelu_p_kernel(tc, x_words, x_scales, w1, w2_words, w2_scal
                     start=True,
                     stop=True,
                 )
-            hidden = keep.tile([P, STEP * PACK], BF16, name=f"hidden{step}", align_bytes=64)
-            nc.scalar.activation(hidden[:].rearrange("p (n t) -> p n t", t=PACK), pre[:].rearrange("p t n -> p n t"), GELU)
-            h_codes = keep.tile([P, STEP], U32, name=f"h_codes{step}", align_bytes=64)
-            h_plane = keep.tile([P, STEP], U8, name=f"h_plane{step}", align_bytes=64)
+            return pre
+
+        def hidden_codes(pre, first, last, name):
+            width = last - first
+            hidden = keep.tile([P, width * PACK], BF16, name=f"hidden{name}", align_bytes=64)
+            nc.scalar.activation(hidden[:].rearrange("p (n t) -> p n t", t=PACK), pre[:, :, first:last].rearrange("p t n -> p n t"), GELU)
+            h_codes = keep.tile([P, width], U32, name=f"h_codes{name}", align_bytes=64)
+            h_plane = keep.tile([P, width], U8, name=f"h_plane{name}", align_bytes=64)
             nc.vector.quantize_mx(out=h_codes[:].bitcast(FP8X4), scales=h_plane[:], in_=hidden[:])
             return h_codes, h_plane
 
@@ -155,12 +159,14 @@ def tile_picked_phmlp_gelu_p_kernel(tc, x_words, x_scales, w1, w2_words, w2_scal
 
         out_rows = out.rearrange("(h p) n -> p h n", p=P)
 
-        def step_result(step):
-            h_codes, h_plane = hidden_codes(step)
-            acc = psum_o.tile([P, 2, STEP], F32, name="acc")
+        def both_halves(codes, width):
+            acc = psum_o.tile([P, 2, width], F32, name="acc")
             for half in range(2):
-                second_product(acc, half, h_codes, h_plane)
+                second_product(acc, half, *codes)
             return acc
+
+        def step_result(step):
+            return both_halves(hidden_codes(first_product(step), 0, STEP, step), STEP)
 
         for first, last in STORE_GROUPS:
             for step in range(first, last):
@@ -170,20 +176,23 @@ def tile_picked_phmlp_gelu_p_kernel(tc, x_words, x_scales, w1, w2_words, w2_scal
                 nc.vector.tensor_copy(group[:, :, (step - first) * STEP : (step - first + 1) * STEP], acc[:])
             nc.sync.dma_start(out_rows[:, :, first * STEP : last * STEP], group[:])
 
-        acc = step_result(STEPS - 2)
-        result = keep.tile([P, 2, STEP], F32, name=f"result{STEPS - 2}", align_bytes=64)
-        nc.scalar.copy(result[:], acc[:])
-        nc.sync.dma_start(out_rows[:, :, S - 2 * STEP : S - STEP], result[:])
+        for step, engine_copy in ((STEPS - 3, nc.scalar.copy), (STEPS - 2, nc.vector.tensor_copy)):
+            acc = step_result(step)
+            result = keep.tile([P, 2, STEP], F32, name=f"result{step}", align_bytes=64)
+            engine_copy(result[:], acc[:])
+            nc.sync.dma_start(out_rows[:, :, step * STEP : (step + 1) * STEP], result[:])
 
-        h_codes, h_plane = hidden_codes(STEPS - 1)
-        halves = []
-        for half in range(2):
-            acc = psum_o.tile([P, 2, STEP], F32, name="acc")
-            second_product(acc, half, h_codes, h_plane)
-            halves.append(acc)
-        cols = slice(S - STEP, S)
+        pre = first_product(STEPS - 1)
+        part = STEP // 2
         result = keep.tile([P, 2, STEP], F32, name=f"result{STEPS - 1}", align_bytes=64)
-        nc.scalar.copy(result[:, 0, :], halves[0][:, 0, :])
-        nc.sync.dma_start(out[0:P, cols], result[:, 0, :])
-        nc.vector.tensor_copy(result[:, 1, :], halves[1][:, 1, :])
-        nc.sync.dma_start(out[P : 2 * P, cols], result[:, 1, :])
+        codes = hidden_codes(pre, 0, part, "part0")
+        acc = psum_h.tile([P, 2, part], F32, name="pre")
+        for half in range(2):
+            second_product(acc, half, *codes)
+        nc.scalar.copy(result[:, :, 0:part], acc[:])
+        codes = hidden_codes(pre, part, STEP, "part1")
+        for half, engine_copy in enumerate((nc.scalar.copy, nc.vector.tensor_copy)):
+            acc = psum_h.tile([P, 2, part], F32, name="pre")
+            second_product(acc, half, *codes)
+            engine_copy(result[:, half, part:STEP], acc[:, half, :])
+        nc.sync.dma_start(out_rows[:, :, S - STEP : S], result[:])

@@ -20,12 +20,13 @@ QUADRANTS = 4
 LIST_ROWS = 16
 STEP = 128
 STEPS = S // STEP
-STORE_GROUPS = ((0, 3), (3, STEPS - 3))
 HALF = H // 2
 SCALAR_SHARE = 32
-EARLY_PLACES = 768
+BANKS = 8
+SLOTS = 3
+LEAD = 6
+EARLY_PLACES = LEAD * STEP
 WORD_GATHERS = (256, 256, 512)
-FIRST_BANKS, SECOND_BANKS = 5, 3
 TENSOR_WARM_UPS = 4
 
 
@@ -33,8 +34,10 @@ def tile_picked_phmlp_gelu_p_kernel(tc, x_words, x_scales, w1, w2_words, w2_scal
     nc = tc.nc
     with ExitStack() as ctx:
         keep = ctx.enter_context(tc.tile_pool(name="keep", bufs=1))
-        psum_h = ctx.enter_context(tc.psum_pool(name="psum_h", bufs=FIRST_BANKS))
-        psum_o = ctx.enter_context(tc.psum_pool(name="psum_o", bufs=SECOND_BANKS))
+        psum = ctx.enter_context(tc.psum_pool(name="psum", bufs=1))
+
+        def bank(number, *shape):
+            return psum.tile([P, *shape], F32, name=f"bank{number}")
 
         offsets = keep.tile([P, S // LIST_ROWS], U16, name="offsets")
 
@@ -52,17 +55,8 @@ def tile_picked_phmlp_gelu_p_kernel(tc, x_words, x_scales, w1, w2_words, w2_scal
 
         nc.sync.dma_start(w1_raw[0][:, 2:PACK, :], w1_rows[:, 2:PACK, 0:HALF])
         nc.sync.dma_start(w1_raw[1][:], w1_rows[:, :, HALF:H])
-
-        w2_plane = keep.tile([P, N], U8, name="w2_plane", align_bytes=64)
-        nc.vector.memset(w2_plane[:].bitcast(I32), 0)
         word_window = keep.tile([P, T], U32, name="word_window", align_bytes=64)
-        for q in range(QUADRANTS):
-            if q == QUADRANTS - 1:
-                nc.sync.dma_start(word_window[:].bitcast(I32), x_words[0].rearrange("p n t -> p (n t)").bitcast(I32))
-            nc.sync.dma_start(w2_plane[32 * q : 32 * q + 4, :].bitcast(I32), w2_scales[0, 4 * q : 4 * q + 4, :].bitcast(I32))
-
-        w2_codes = keep.tile([P, N], U32, name="w2_codes", align_bytes=64)
-        nc.sync.dma_start(w2_codes[:].bitcast(I32), w2_words[0].rearrange("p n t -> p (n t)").bitcast(I32))
+        nc.sync.dma_start(word_window[:].bitcast(I32), x_words[0].rearrange("p n t -> p (n t)").bitcast(I32))
 
         warm = keep.tile([P, 2], F32, name="warm")
         nc.vector.memset(warm[:, 0:1], 0.0)
@@ -70,6 +64,8 @@ def tile_picked_phmlp_gelu_p_kernel(tc, x_words, x_scales, w1, w2_words, w2_scal
 
         x_plane = keep.tile([P, S], U8, name="x_plane", align_bytes=64)
         nc.vector.memset(x_plane[:].bitcast(I32), 0)
+        w2_plane = keep.tile([P, N], U8, name="w2_plane", align_bytes=64)
+        nc.vector.memset(w2_plane[:].bitcast(I32), 0)
 
         def pick_scales(picked, first, last):
             nc.vector.tensor_copy(picked[:], scale_window[:].indirect(entries(first, last)))
@@ -83,6 +79,11 @@ def tile_picked_phmlp_gelu_p_kernel(tc, x_words, x_scales, w1, w2_words, w2_scal
         pick_scales(early_scales, 0, EARLY_PLACES)
         late_scales = keep.tile([P, S - EARLY_PLACES], U8, name="late_scales", align_bytes=64)
         pick_scales(late_scales, EARLY_PLACES, S)
+
+        w2_codes = keep.tile([P, N], U32, name="w2_codes", align_bytes=64)
+        nc.sync.dma_start(w2_codes[:].bitcast(I32), w2_words[0].rearrange("p n t -> p (n t)").bitcast(I32))
+        for q in range(QUADRANTS):
+            nc.sync.dma_start(w2_plane[32 * q : 32 * q + 4, :].bitcast(I32), w2_scales[0, 4 * q : 4 * q + 4, :].bitcast(I32))
 
         w1_grouped = keep.tile([P, H * PACK], BF16, name="w1_grouped", align_bytes=64)
         groups = HALF // PACK
@@ -104,7 +105,7 @@ def tile_picked_phmlp_gelu_p_kernel(tc, x_words, x_scales, w1, w2_words, w2_scal
                 in_=w1_grouped[:, t * P * PACK : (t + 1) * P * PACK],
             )
 
-        heat = psum_o.tile([P, 2 * P], F32, name="acc")
+        heat = bank(BANKS - 1, 2 * P)
         for repeat in range(TENSOR_WARM_UPS):
             nc.tensor.matmul_mx(
                 out=heat[:],
@@ -124,7 +125,7 @@ def tile_picked_phmlp_gelu_p_kernel(tc, x_words, x_scales, w1, w2_words, w2_scal
 
         def first_product(step):
             cols = slice(step * STEP, (step + 1) * STEP)
-            pre = psum_h.tile([P, PACK, STEP], F32, name="pre")
+            pre = bank(step, PACK, STEP)
             for t in range(PACK):
                 nc.tensor.matmul_mx(
                     out=pre[:, t, :],
@@ -137,18 +138,20 @@ def tile_picked_phmlp_gelu_p_kernel(tc, x_words, x_scales, w1, w2_words, w2_scal
                 )
             return pre
 
-        def hidden_codes(pre, first, last, name):
-            width = last - first
-            hidden = keep.tile([P, width * PACK], BF16, name=f"hidden{name}", align_bytes=64)
+        def gelu(pre, first, last, name):
+            hidden = keep.tile([P, (last - first) * PACK], BF16, name=name, align_bytes=64)
             nc.scalar.activation(hidden[:].rearrange("p (n t) -> p n t", t=PACK), pre[:, :, first:last].rearrange("p t n -> p n t"), GELU)
-            h_codes = keep.tile([P, width], U32, name=f"h_codes{name}", align_bytes=64)
-            h_plane = keep.tile([P, width], U8, name=f"h_plane{name}", align_bytes=64)
+            return hidden
+
+        def quantise(hidden, width, codes_name, plane_name):
+            h_codes = keep.tile([P, width], U32, name=codes_name, align_bytes=64)
+            h_plane = keep.tile([P, width], U8, name=plane_name, align_bytes=64)
             nc.vector.quantize_mx(out=h_codes[:].bitcast(FP8X4), scales=h_plane[:], in_=hidden[:])
             return h_codes, h_plane
 
         def second_product(acc, half, h_codes, h_plane):
             nc.tensor.matmul_mx(
-                out=acc[:, half, :],
+                out=acc,
                 lhsT=w2_codes[:, half * P : (half + 1) * P].bitcast(FP8X4),
                 lhsT_scale=w2_plane[:, half * P : (half + 1) * P],
                 rhs=h_codes[:].bitcast(FP8X4),
@@ -157,42 +160,55 @@ def tile_picked_phmlp_gelu_p_kernel(tc, x_words, x_scales, w1, w2_words, w2_scal
                 stop=True,
             )
 
-        out_rows = out.rearrange("(h p) n -> p h n", p=P)
-
-        def both_halves(codes, width):
-            acc = psum_o.tile([P, 2, width], F32, name="acc")
+        def both_halves(number, codes, width):
+            acc = bank(number, 2, width)
             for half in range(2):
-                second_product(acc, half, *codes)
+                second_product(acc[:, half, :], half, *codes)
             return acc
 
-        def step_result(step):
-            return both_halves(hidden_codes(first_product(step), 0, STEP, step), STEP)
-
-        for first, last in STORE_GROUPS:
+        out_rows = out.rearrange("(h p) n -> p h n", p=P)
+        stores = ((0, 3), (3, 5), (5, 6), (6, 7), (7, 8))
+        staged = {}
+        for first, last in stores:
+            tile = keep.tile([P, 2, (last - first) * STEP], F32, name=f"result{first}", align_bytes=64)
             for step in range(first, last):
-                acc = step_result(step)
-                if step == first:
-                    group = keep.tile([P, 2, (last - first) * STEP], F32, name=f"result{step}", align_bytes=64)
-                nc.vector.tensor_copy(group[:, :, (step - first) * STEP : (step - first + 1) * STEP], acc[:])
-            nc.sync.dma_start(out_rows[:, :, first * STEP : last * STEP], group[:])
+                staged[step] = (tile, first, last)
 
-        for step, engine_copy in ((STEPS - 3, nc.scalar.copy), (STEPS - 2, nc.vector.tensor_copy)):
-            acc = step_result(step)
-            result = keep.tile([P, 2, STEP], F32, name=f"result{step}", align_bytes=64)
-            engine_copy(result[:], acc[:])
-            nc.sync.dma_start(out_rows[:, :, step * STEP : (step + 1) * STEP], result[:])
+        def copy_out(step, acc, engine_copy):
+            tile, first, last = staged[step]
+            engine_copy(tile[:, :, (step - first) * STEP : (step - first + 1) * STEP], acc[:])
+            if step == last - 1:
+                nc.sync.dma_start(out_rows[:, :, first * STEP : last * STEP], tile[:])
 
-        pre = first_product(STEPS - 1)
+        hidden = {}
+        for step in range(LEAD):
+            hidden[step] = gelu(first_product(step), 0, STEP, f"hidden{step}")
+
+        def step_acc(step):
+            codes = quantise(hidden[step], STEP, f"h_codes{step}", f"h_plane{step % SLOTS}")
+            return both_halves((LEAD + step) % BANKS, codes, STEP)
+
         part = STEP // 2
-        result = keep.tile([P, 2, STEP], F32, name=f"result{STEPS - 1}", align_bytes=64)
-        codes = hidden_codes(pre, 0, part, "part0")
-        acc = psum_h.tile([P, 2, part], F32, name="pre")
-        for half in range(2):
-            second_product(acc, half, *codes)
-        nc.scalar.copy(result[:, :, 0:part], acc[:])
-        codes = hidden_codes(pre, part, STEP, "part1")
+        last_step = STEPS - 1
+        acc = {}
+        for step in range(last_step):
+            acc[step] = step_acc(step)
+            if step >= 2:
+                copy_out(step - 2, acc[step - 2], nc.vector.tensor_copy)
+            if step == 2:
+                hidden[LEAD] = gelu(first_product(LEAD), 0, STEP, f"hidden{LEAD}")
+            if step == 3:
+                pre = first_product(last_step)
+                parts = [gelu(pre, 0, part, "hidden_part0"), gelu(pre, part, STEP, "hidden_part1")]
+
+        result = staged[last_step][0]
+        codes0 = quantise(parts[0], part, "h_codes_part0", f"h_plane{last_step % SLOTS}")
+        codes1 = quantise(parts[1], part, "h_codes_part1", f"h_plane{(last_step + 1) % SLOTS}")
+        copy_out(last_step - 2, acc[last_step - 2], nc.scalar.copy)
+        copy_out(last_step - 1, acc[last_step - 1], nc.vector.tensor_copy)
+        nc.scalar.copy(result[:, :, 0:part], both_halves(5, codes0, part)[:])
         for half, engine_copy in enumerate((nc.scalar.copy, nc.vector.tensor_copy)):
-            acc = psum_h.tile([P, 2, part], F32, name="pre")
-            second_product(acc, half, *codes)
-            engine_copy(result[:, half, part:STEP], acc[:, half, :])
+            last = bank(half, part)
+            second_product(last[:], half, *codes1)
+            engine_copy(result[:, half, part:STEP], last[:])
         nc.sync.dma_start(out_rows[:, :, S - STEP : S], result[:])

@@ -62,28 +62,17 @@ def tile_picked_phmlp_gelu_p_kernel(tc, x_words, x_scales, w1, w2_words, w2_scal
         nc.vector.memset(warm[:, 0:1], 0.0)
         nc.scalar.activation(warm[:, 1:2], warm[:, 0:1], GELU)
 
-        x_plane = keep.tile([P, S], U8, name="x_plane", align_bytes=64)
+        x_plane = keep.tile([P, EARLY_PLACES], U8, name="x_plane", align_bytes=64)
         nc.vector.memset(x_plane[:].bitcast(I32), 0)
         w2_plane = keep.tile([P, N], U8, name="w2_plane", align_bytes=64)
         nc.vector.memset(w2_plane[:].bitcast(I32), 0)
 
-        def pick_scales(picked, first, last):
-            nc.vector.tensor_copy(picked[:], scale_window[:].indirect(entries(first, last)))
-            for q in range(QUADRANTS):
-                nc.sync.dma_start(
-                    x_plane[32 * q : 32 * q + 4, first:last].bitcast(I32),
-                    picked[32 * q : 32 * q + 32 : 8, :].bitcast(I32),
-                )
-
         early_scales = keep.tile([P, EARLY_PLACES], U8, name="early_scales", align_bytes=64)
-        pick_scales(early_scales, 0, EARLY_PLACES)
-        late_scales = keep.tile([P, S - EARLY_PLACES], U8, name="late_scales", align_bytes=64)
-        pick_scales(late_scales, EARLY_PLACES, S)
-
-        w2_codes = keep.tile([P, N], U32, name="w2_codes", align_bytes=64)
-        nc.sync.dma_start(w2_codes[:].bitcast(I32), w2_words[0].rearrange("p n t -> p (n t)").bitcast(I32))
+        nc.vector.tensor_copy(early_scales[:], scale_window[:].indirect(entries(0, EARLY_PLACES)))
         for q in range(QUADRANTS):
-            nc.sync.dma_start(w2_plane[32 * q : 32 * q + 4, :].bitcast(I32), w2_scales[0, 4 * q : 4 * q + 4, :].bitcast(I32))
+            nc.sync.dma_start(x_plane[32 * q : 32 * q + 4, :].bitcast(I32), early_scales[32 * q : 32 * q + 32 : 8, :].bitcast(I32))
+        late_scales = keep.tile([P, S - EARLY_PLACES], U8, name="late_scales", align_bytes=64)
+        nc.vector.tensor_copy(late_scales[:], scale_window[:].indirect(entries(EARLY_PLACES, S)))
 
         w1_grouped = keep.tile([P, H * PACK], BF16, name="w1_grouped", align_bytes=64)
         groups = HALF // PACK
@@ -105,6 +94,16 @@ def tile_picked_phmlp_gelu_p_kernel(tc, x_words, x_scales, w1, w2_words, w2_scal
                 in_=w1_grouped[:, t * P * PACK : (t + 1) * P * PACK],
             )
 
+        late_plane = keep.tile([P, S - EARLY_PLACES], U8, name="w1_grouped", align_bytes=64)
+        nc.vector.tensor_copy(late_plane[:].bitcast(I32), late_scales[:].bitcast(I32))
+        for row in range(1, 4):
+            nc.sync.dma_start(late_plane[row:P:32, :].bitcast(I32), late_scales[8 * row : P : 32, :].bitcast(I32))
+
+        w2_codes = keep.tile([P, N], U32, name="w2_codes", align_bytes=64)
+        nc.sync.dma_start(w2_codes[:].bitcast(I32), w2_words[0].rearrange("p n t -> p (n t)").bitcast(I32))
+        for q in range(QUADRANTS):
+            nc.sync.dma_start(w2_plane[32 * q : 32 * q + 4, :].bitcast(I32), w2_scales[0, 4 * q : 4 * q + 4, :].bitcast(I32))
+
         heat = bank(BANKS - 1, 2 * P)
         for repeat in range(TENSOR_WARM_UPS):
             nc.tensor.matmul_mx(
@@ -125,6 +124,7 @@ def tile_picked_phmlp_gelu_p_kernel(tc, x_words, x_scales, w1, w2_words, w2_scal
 
         def first_product(step):
             cols = slice(step * STEP, (step + 1) * STEP)
+            plane = x_plane[:, cols] if step < LEAD else late_plane[:, (step - LEAD) * STEP : (step - LEAD + 1) * STEP]
             pre = bank(step, PACK, STEP)
             for t in range(PACK):
                 nc.tensor.matmul_mx(
@@ -132,7 +132,7 @@ def tile_picked_phmlp_gelu_p_kernel(tc, x_words, x_scales, w1, w2_words, w2_scal
                     lhsT=w1_codes[:, t * P : (t + 1) * P].bitcast(FP8X4),
                     lhsT_scale=w1_plane[:, t * P : (t + 1) * P],
                     rhs=picked_words[:, cols].bitcast(FP8X4),
-                    rhs_scale=x_plane[:, cols],
+                    rhs_scale=plane,
                     start=True,
                     stop=True,
                 )
@@ -167,7 +167,7 @@ def tile_picked_phmlp_gelu_p_kernel(tc, x_words, x_scales, w1, w2_words, w2_scal
             return acc
 
         out_rows = out.rearrange("(h p) n -> p h n", p=P)
-        stores = ((0, 3), (3, 5), (5, 6), (6, 7), (7, 8))
+        stores = ((0, 2), (2, 4), (4, 5), (5, 6), (6, 7), (7, 8))
         staged = {}
         for first, last in stores:
             tile = keep.tile([P, 2, (last - first) * STEP], F32, name=f"result{first}", align_bytes=64)
@@ -192,7 +192,13 @@ def tile_picked_phmlp_gelu_p_kernel(tc, x_words, x_scales, w1, w2_words, w2_scal
         last_step = STEPS - 1
         acc = {}
         for step in range(last_step):
-            acc[step] = step_acc(step)
+            if step < last_step - 2:
+                acc[step] = step_acc(step)
+            else:
+                codes = quantise(hidden[step], STEP, f"h_codes{step}", f"h_plane{step % SLOTS}")
+                acc[step] = [bank(number, STEP) for number in ((3, 5), (4, 6))[step - last_step + 2]]
+                for half in range(2):
+                    second_product(acc[step][half][:], half, *codes)
             if step >= 2:
                 copy_out(step - 2, acc[step - 2], nc.vector.tensor_copy)
             if step == 2:
@@ -204,11 +210,13 @@ def tile_picked_phmlp_gelu_p_kernel(tc, x_words, x_scales, w1, w2_words, w2_scal
         result = staged[last_step][0]
         codes0 = quantise(parts[0], part, "h_codes_part0", f"h_plane{last_step % SLOTS}")
         codes1 = quantise(parts[1], part, "h_codes_part1", f"h_plane{(last_step + 1) % SLOTS}")
-        copy_out(last_step - 2, acc[last_step - 2], nc.scalar.copy)
-        copy_out(last_step - 1, acc[last_step - 1], nc.vector.tensor_copy)
-        nc.scalar.copy(result[:, :, 0:part], both_halves(5, codes0, part)[:])
-        for half, engine_copy in enumerate((nc.scalar.copy, nc.vector.tensor_copy)):
-            last = bank(half, part)
-            second_product(last[:], half, *codes1)
-            engine_copy(result[:, half, part:STEP], last[:])
+        for step in (last_step - 2, last_step - 1):
+            for half, engine_copy in enumerate((nc.scalar.copy, nc.vector.tensor_copy)):
+                engine_copy(staged[step][0][:, half, :], acc[step][half][:])
+            nc.sync.dma_start(out_rows[:, :, step * STEP : (step + 1) * STEP], staged[step][0][:])
+        for first, codes, banks in ((0, codes0, (0, 1)), (part, codes1, (2, 7))):
+            for half, engine_copy in enumerate((nc.scalar.copy, nc.vector.tensor_copy)):
+                last = bank(banks[half], part)
+                second_product(last[:], half, *codes)
+                engine_copy(result[:, half, first : first + part], last[:])
         nc.sync.dma_start(out_rows[:, :, S - STEP : S], result[:])

@@ -25,7 +25,7 @@ SCALAR_SHARE = 32
 BANKS = 8
 SLOTS = 3
 LEAD = 6
-EARLY_PLACES = LEAD * STEP
+EARLY_PLACES = 512
 WORD_GATHERS = (256, 256, 512)
 TENSOR_WARM_UPS = 4
 
@@ -124,7 +124,7 @@ def tile_picked_phmlp_gelu_p_kernel(tc, x_words, x_scales, w1, w2_words, w2_scal
 
         def first_product(step):
             cols = slice(step * STEP, (step + 1) * STEP)
-            plane = x_plane[:, cols] if step < LEAD else late_plane[:, (step - LEAD) * STEP : (step - LEAD + 1) * STEP]
+            plane = x_plane[:, cols] if cols.start < EARLY_PLACES else late_plane[:, cols.start - EARLY_PLACES : cols.stop - EARLY_PLACES]
             pre = bank(step, PACK, STEP)
             for t in range(PACK):
                 nc.tensor.matmul_mx(

@@ -17,16 +17,22 @@ GELU = mybir.ActivationFunctionType.Gelu_apprx_tanh
 P = 128
 PACK = 4
 QUADRANTS = 4
+PLANE_ROWS = 4
 LIST_ROWS = 16
 STEP = 128
 STEPS = S // STEP
 HALF = H // 2
-SCALAR_SHARE = 32
+LEAD_ROWS = 3
 BANKS = 8
-SLOTS = 3
 LEAD = 6
-EARLY_PLACES = 512
+LAG = 2
+SLOTS = LAG + 1
+EARLY_PLACES = S // 2
 WORD_GATHERS = (256, 256, 512)
+STORE_GROUPS = ((0, 2), (2, 4), (4, 5), (5, 6), (6, 7), (7, 8))
+SPLIT_FROM = 5
+SPLIT_BANKS = ((3, 5), (4, 6))
+PART_BANKS = ((0, 1), (2, 7))
 TENSOR_WARM_UPS = 4
 
 
@@ -46,14 +52,14 @@ def tile_picked_phmlp_gelu_p_kernel(tc, x_words, x_scales, w1, w2_words, w2_scal
 
         w1_rows = w1.rearrange("(p j) c -> p j c", j=PACK)
         w1_raw = [keep.tile([P, PACK, HALF], F32, name=f"w1_raw{half}") for half in range(2)]
-        nc.sync.dma_start(w1_raw[0][:, 0:2, :], w1_rows[:, 0:2, 0:HALF])
+        nc.sync.dma_start(w1_raw[0][:, 0:LEAD_ROWS, :], w1_rows[:, 0:LEAD_ROWS, 0:HALF])
         nc.sync.dma_start(offsets[:], offs)
 
         scale_window = keep.tile([P, T], U8, name="scale_window", align_bytes=64)
         nc.vector.memset(scale_window[:].bitcast(I32), 0)
         nc.sync.dma_start(scale_window[0:P:8, :].bitcast(I32), x_scales[0].bitcast(I32))
 
-        nc.sync.dma_start(w1_raw[0][:, 2:PACK, :], w1_rows[:, 2:PACK, 0:HALF])
+        nc.sync.dma_start(w1_raw[0][:, LEAD_ROWS:PACK, :], w1_rows[:, LEAD_ROWS:PACK, 0:HALF])
         nc.sync.dma_start(w1_raw[1][:], w1_rows[:, :, HALF:H])
         word_window = keep.tile([P, T], U32, name="word_window", align_bytes=64)
         nc.sync.dma_start(word_window[:].bitcast(I32), x_words[0].rearrange("p n t -> p (n t)").bitcast(I32))
@@ -82,9 +88,8 @@ def tile_picked_phmlp_gelu_p_kernel(tc, x_words, x_scales, w1, w2_words, w2_scal
         )
         grouped_view = w1_grouped[:].rearrange("p (u e m j) -> p u m j e", u=2, e=2, j=PACK)
         raw_view = w1_raw[1][:].rearrange("p j (m u e) -> p u m j e", u=2, e=2)
-        nc.scalar.copy(grouped_view[:, 0, groups:P], raw_view[:, 0])
-        nc.scalar.copy(grouped_view[:, 1, groups : groups + SCALAR_SHARE], raw_view[:, 1, 0:SCALAR_SHARE])
-        nc.vector.tensor_copy(grouped_view[:, 1, groups + SCALAR_SHARE : P], raw_view[:, 1, SCALAR_SHARE:groups])
+        for pair in range(2):
+            nc.scalar.copy(grouped_view[:, pair, groups:P], raw_view[:, pair])
         w1_codes = keep.tile([P, H], U32, name="w1_codes", align_bytes=64)
         w1_plane = keep.tile([P, H], U8, name="w1_plane", align_bytes=64)
         for t in range(PACK):
@@ -96,7 +101,7 @@ def tile_picked_phmlp_gelu_p_kernel(tc, x_words, x_scales, w1, w2_words, w2_scal
 
         late_plane = keep.tile([P, S - EARLY_PLACES], U8, name="w1_grouped", align_bytes=64)
         nc.vector.tensor_copy(late_plane[:].bitcast(I32), late_scales[:].bitcast(I32))
-        for row in range(1, 4):
+        for row in range(1, PLANE_ROWS):
             nc.sync.dma_start(late_plane[row:P:32, :].bitcast(I32), late_scales[8 * row : P : 32, :].bitcast(I32))
 
         w2_codes = keep.tile([P, N], U32, name="w2_codes", align_bytes=64)
@@ -139,19 +144,19 @@ def tile_picked_phmlp_gelu_p_kernel(tc, x_words, x_scales, w1, w2_words, w2_scal
             return pre
 
         def gelu(pre, first, last, name):
-            hidden = keep.tile([P, (last - first) * PACK], BF16, name=name, align_bytes=64)
-            nc.scalar.activation(hidden[:].rearrange("p (n t) -> p n t", t=PACK), pre[:, :, first:last].rearrange("p t n -> p n t"), GELU)
-            return hidden
+            h_values = keep.tile([P, (last - first) * PACK], BF16, name=name, align_bytes=64)
+            nc.scalar.activation(h_values[:].rearrange("p (n t) -> p n t", t=PACK), pre[:, :, first:last].rearrange("p t n -> p n t"), GELU)
+            return h_values
 
-        def quantise(hidden, width, codes_name, plane_name):
-            h_codes = keep.tile([P, width], U32, name=codes_name, align_bytes=64)
-            h_plane = keep.tile([P, width], U8, name=plane_name, align_bytes=64)
-            nc.vector.quantize_mx(out=h_codes[:].bitcast(FP8X4), scales=h_plane[:], in_=hidden[:])
+        def quantise(h_values, width, name, turn):
+            h_codes = keep.tile([P, width], U32, name=name, align_bytes=64)
+            h_plane = keep.tile([P, width], U8, name=f"h_plane{turn % SLOTS}", align_bytes=64)
+            nc.vector.quantize_mx(out=h_codes[:].bitcast(FP8X4), scales=h_plane[:], in_=h_values[:])
             return h_codes, h_plane
 
-        def second_product(acc, half, h_codes, h_plane):
+        def second_product(target, half, h_codes, h_plane):
             nc.tensor.matmul_mx(
-                out=acc,
+                out=target,
                 lhsT=w2_codes[:, half * P : (half + 1) * P].bitcast(FP8X4),
                 lhsT_scale=w2_plane[:, half * P : (half + 1) * P],
                 rhs=h_codes[:].bitcast(FP8X4),
@@ -160,63 +165,55 @@ def tile_picked_phmlp_gelu_p_kernel(tc, x_words, x_scales, w1, w2_words, w2_scal
                 stop=True,
             )
 
-        def both_halves(number, codes, width):
-            acc = bank(number, 2, width)
-            for half in range(2):
-                second_product(acc[:, half, :], half, *codes)
-            return acc
-
         out_rows = out.rearrange("(h p) n -> p h n", p=P)
-        stores = ((0, 2), (2, 4), (4, 5), (5, 6), (6, 7), (7, 8))
         staged = {}
-        for first, last in stores:
-            tile = keep.tile([P, 2, (last - first) * STEP], F32, name=f"result{first}", align_bytes=64)
+        for first, last in STORE_GROUPS:
+            group = keep.tile([P, 2, (last - first) * STEP], F32, name=f"result{first}", align_bytes=64)
             for step in range(first, last):
-                staged[step] = (tile, first, last)
+                staged[step] = (group, first, last)
 
-        def copy_out(step, acc, engine_copy):
-            tile, first, last = staged[step]
-            engine_copy(tile[:, :, (step - first) * STEP : (step - first + 1) * STEP], acc[:])
+        def store_if_complete(step):
+            group, first, last = staged[step]
             if step == last - 1:
-                nc.sync.dma_start(out_rows[:, :, first * STEP : last * STEP], tile[:])
+                nc.sync.dma_start(out_rows[:, :, first * STEP : last * STEP], group[:])
 
         hidden = {}
         for step in range(LEAD):
             hidden[step] = gelu(first_product(step), 0, STEP, f"hidden{step}")
 
-        def step_acc(step):
-            codes = quantise(hidden[step], STEP, f"h_codes{step}", f"h_plane{step % SLOTS}")
-            return both_halves((LEAD + step) % BANKS, codes, STEP)
-
         part = STEP // 2
         last_step = STEPS - 1
         acc = {}
         for step in range(last_step):
-            if step < last_step - 2:
-                acc[step] = step_acc(step)
+            codes = quantise(hidden[step], STEP, f"h_codes{step}", step)
+            if step < SPLIT_FROM:
+                acc[step] = bank((LEAD + step) % BANKS, 2, STEP)
+                targets = [acc[step][:, half, :] for half in range(2)]
             else:
-                codes = quantise(hidden[step], STEP, f"h_codes{step}", f"h_plane{step % SLOTS}")
-                acc[step] = [bank(number, STEP) for number in ((3, 5), (4, 6))[step - last_step + 2]]
-                for half in range(2):
-                    second_product(acc[step][half][:], half, *codes)
-            if step >= 2:
-                copy_out(step - 2, acc[step - 2], nc.vector.tensor_copy)
-            if step == 2:
+                acc[step] = [bank(number, STEP) for number in SPLIT_BANKS[step - SPLIT_FROM]]
+                targets = [tile[:] for tile in acc[step]]
+            for half in range(2):
+                second_product(targets[half], half, *codes)
+            done = step - LAG
+            if done >= 0:
+                group, first, last = staged[done]
+                nc.vector.tensor_copy(group[:, :, (done - first) * STEP : (done - first + 1) * STEP], acc[done][:])
+                store_if_complete(done)
+            if done == 0:
                 hidden[LEAD] = gelu(first_product(LEAD), 0, STEP, f"hidden{LEAD}")
-            if step == 3:
+            if done == 1:
                 pre = first_product(last_step)
                 parts = [gelu(pre, 0, part, "hidden_part0"), gelu(pre, part, STEP, "hidden_part1")]
 
-        result = staged[last_step][0]
-        codes0 = quantise(parts[0], part, "h_codes_part0", f"h_plane{last_step % SLOTS}")
-        codes1 = quantise(parts[1], part, "h_codes_part1", f"h_plane{(last_step + 1) % SLOTS}")
-        for step in (last_step - 2, last_step - 1):
-            for half, engine_copy in enumerate((nc.scalar.copy, nc.vector.tensor_copy)):
+        part_codes = [quantise(parts[number], part, f"h_codes_part{number}", last_step + number) for number in range(2)]
+        engine_copies = (nc.scalar.copy, nc.vector.tensor_copy)
+        for step in range(SPLIT_FROM, last_step):
+            for half, engine_copy in enumerate(engine_copies):
                 engine_copy(staged[step][0][:, half, :], acc[step][half][:])
-            nc.sync.dma_start(out_rows[:, :, step * STEP : (step + 1) * STEP], staged[step][0][:])
-        for first, codes, banks in ((0, codes0, (0, 1)), (part, codes1, (2, 7))):
-            for half, engine_copy in enumerate((nc.scalar.copy, nc.vector.tensor_copy)):
-                last = bank(banks[half], part)
-                second_product(last[:], half, *codes)
-                engine_copy(result[:, half, first : first + part], last[:])
-        nc.sync.dma_start(out_rows[:, :, S - STEP : S], result[:])
+            store_if_complete(step)
+        for number, codes in enumerate(part_codes):
+            for half, engine_copy in enumerate(engine_copies):
+                part_acc = bank(PART_BANKS[number][half], part)
+                second_product(part_acc[:], half, *codes)
+                engine_copy(staged[last_step][0][:, half, number * part : (number + 1) * part], part_acc[:])
+        store_if_complete(last_step)

@@ -33,7 +33,7 @@ STORE_GROUPS = ((0, 2), (2, 4), (4, 5), (5, 6), (6, 7), (7, 8))
 SPLIT_FROM = 5
 SPLIT_BANKS = ((3, 5), (4, 6))
 PART_BANKS = ((0, 1), (2, 7))
-TENSOR_WARM_UPS = 4
+TENSOR_WARM_UPS = 2
 
 
 def tile_picked_phmlp_gelu_p_kernel(tc, x_words, x_scales, w1, w2_words, w2_scales, offs, out):
@@ -113,10 +113,10 @@ def tile_picked_phmlp_gelu_p_kernel(tc, x_words, x_scales, w1, w2_words, w2_scal
         for repeat in range(TENSOR_WARM_UPS):
             nc.tensor.matmul_mx(
                 out=heat[:],
-                lhsT=w1_codes[:, 0:P].bitcast(FP8X4),
-                lhsT_scale=w1_plane[:, 0:P],
-                rhs=w1_codes[:, 0 : 2 * P].bitcast(FP8X4),
-                rhs_scale=w1_plane[:, 0 : 2 * P],
+                lhsT=w1_codes[:, 2 * P : 3 * P].bitcast(FP8X4),
+                lhsT_scale=w1_plane[:, 2 * P : 3 * P],
+                rhs=w1_codes[:, 2 * P : H].bitcast(FP8X4),
+                rhs_scale=w1_plane[:, 2 * P : H],
                 start=True,
                 stop=True,
             )

@@ -33,7 +33,8 @@ STORE_GROUPS = ((0, 2), (2, 4), (4, 5), (5, 6), (6, 7), (7, 8))
 SPLIT_FROM = 5
 SPLIT_BANKS = ((3, 5), (4, 6))
 PART_BANKS = ((0, 1), (2, 7))
-TENSOR_WARM_UPS = 2
+TENSOR_WARM_UPS = (128, 128, 128, 128, 512)
+WARM_UP_ROWS = 32
 
 
 def tile_picked_phmlp_gelu_p_kernel(tc, x_words, x_scales, w1, w2_words, w2_scales, offs, out):
@@ -109,14 +110,14 @@ def tile_picked_phmlp_gelu_p_kernel(tc, x_words, x_scales, w1, w2_words, w2_scal
         for q in range(QUADRANTS):
             nc.sync.dma_start(w2_plane[32 * q : 32 * q + 4, :].bitcast(I32), w2_scales[0, 4 * q : 4 * q + 4, :].bitcast(I32))
 
-        heat = bank(BANKS - 1, 2 * P)
-        for repeat in range(TENSOR_WARM_UPS):
+        heat = psum.tile([WARM_UP_ROWS, H], F32, name=f"bank{BANKS - 1}")
+        for width in TENSOR_WARM_UPS:
             nc.tensor.matmul_mx(
-                out=heat[:],
-                lhsT=w1_codes[:, 2 * P : 3 * P].bitcast(FP8X4),
-                lhsT_scale=w1_plane[:, 2 * P : 3 * P],
-                rhs=w1_codes[:, 2 * P : H].bitcast(FP8X4),
-                rhs_scale=w1_plane[:, 2 * P : H],
+                out=heat[:, 0:width],
+                lhsT=w1_codes[:, 0:WARM_UP_ROWS].bitcast(FP8X4),
+                lhsT_scale=w1_plane[:, 0:WARM_UP_ROWS],
+                rhs=w1_codes[:, 0:width].bitcast(FP8X4),
+                rhs_scale=w1_plane[:, 0:width],
                 start=True,
                 stop=True,
             )

@@ -52,7 +52,7 @@ def tile_picked_phmlp_gelu_p_kernel(tc, x_words, x_scales, w1, w2_words, w2_scal
             return offsets[:, first // LIST_ROWS : last // LIST_ROWS]
 
         w1_rows = w1.rearrange("(p j) c -> p j c", j=PACK)
-        w1_raw = [keep.tile([P, PACK, HALF], F32, name=f"w1_raw{half}") for half in range(2)]
+        w1_raw = [keep.tile([P, PACK, HALF], F32, name=f"w1_raw{half}", align_bytes=64) for half in range(2)]
         nc.sync.dma_start(w1_raw[0][:, 0:LEAD_ROWS, :], w1_rows[:, 0:LEAD_ROWS, 0:HALF])
         nc.sync.dma_start(offsets[:], offs)
 
@@ -100,7 +100,7 @@ def tile_picked_phmlp_gelu_p_kernel(tc, x_words, x_scales, w1, w2_words, w2_scal
                 in_=w1_grouped[:, t * P * PACK : (t + 1) * P * PACK],
             )
 
-        late_plane = keep.tile([P, S - EARLY_PLACES], U8, name="w1_grouped", align_bytes=64)
+        late_plane = keep.tile([P, S - EARLY_PLACES], U8, name="w1_raw1", align_bytes=64)
         nc.vector.tensor_copy(late_plane[:].bitcast(I32), late_scales[:].bitcast(I32))
         for row in range(1, PLANE_ROWS):
             nc.sync.dma_start(late_plane[row:P:32, :].bitcast(I32), late_scales[8 * row : P : 32, :].bitcast(I32))

@@ -93,11 +93,11 @@ def tile_picked_phmlp_gelu_p_kernel(tc, x_words, x_scales, w1, w2_words, w2_scal
             nc.scalar.copy(grouped_view[:, pair, groups:P], raw_view[:, pair])
         w1_codes = keep.tile([P, H], U32, name="w1_codes", align_bytes=64)
         w1_plane = keep.tile([P, H], U8, name="w1_plane", align_bytes=64)
-        for t in range(PACK):
+        for pair in range(2):
             nc.vector.quantize_mx(
-                out=w1_codes[:, t * P : (t + 1) * P].bitcast(FP8X4),
-                scales=w1_plane[:, t * P : (t + 1) * P],
-                in_=w1_grouped[:, t * P * PACK : (t + 1) * P * PACK],
+                out=w1_codes[:, pair * HALF : (pair + 1) * HALF].bitcast(FP8X4),
+                scales=w1_plane[:, pair * HALF : (pair + 1) * HALF],
+                in_=w1_grouped[:, pair * HALF * PACK : (pair + 1) * HALF * PACK],
             )
 
         late_plane = keep.tile([P, S - EARLY_PLACES], U8, name="w1_raw1", align_bytes=64)

@@ -15,6 +15,7 @@ FP8X4 = mybir.dt.float8_e4m3fn_x4
 GELU = mybir.ActivationFunctionType.Gelu_apprx_tanh
 
 P = 128
+ALIGN = 256
 PACK = 4
 QUADRANTS = 4
 PLANE_ROWS = 4
@@ -46,42 +47,42 @@ def tile_picked_phmlp_gelu_p_kernel(tc, x_words, x_scales, w1, w2_words, w2_scal
         def bank(number, *shape):
             return psum.tile([P, *shape], F32, name=f"bank{number}")
 
-        offsets = keep.tile([P, S // LIST_ROWS], U16, name="offsets")
+        offsets = keep.tile([P, S // LIST_ROWS], U16, name="offsets", align_bytes=ALIGN)
 
         def entries(first, last):
             return offsets[:, first // LIST_ROWS : last // LIST_ROWS]
 
         w1_rows = w1.rearrange("(p j) c -> p j c", j=PACK)
-        w1_raw = [keep.tile([P, PACK, HALF], F32, name=f"w1_raw{half}", align_bytes=64) for half in range(2)]
+        w1_raw = [keep.tile([P, PACK, HALF], F32, name=f"w1_raw{half}", align_bytes=ALIGN) for half in range(2)]
         nc.sync.dma_start(w1_raw[0][:, 0:LEAD_ROWS, :], w1_rows[:, 0:LEAD_ROWS, 0:HALF])
         nc.sync.dma_start(offsets[:], offs)
 
-        scale_window = keep.tile([P, T], U8, name="scale_window", align_bytes=64)
+        scale_window = keep.tile([P, T], U8, name="scale_window", align_bytes=ALIGN)
         nc.vector.memset(scale_window[:].bitcast(I32), 0)
         nc.sync.dma_start(scale_window[0:P:8, :].bitcast(I32), x_scales[0].bitcast(I32))
 
         nc.sync.dma_start(w1_raw[0][:, LEAD_ROWS:PACK, :], w1_rows[:, LEAD_ROWS:PACK, 0:HALF])
         nc.sync.dma_start(w1_raw[1][:], w1_rows[:, :, HALF:H])
-        word_window = keep.tile([P, T], U32, name="word_window", align_bytes=64)
+        word_window = keep.tile([P, T], U32, name="word_window", align_bytes=ALIGN)
         nc.sync.dma_start(word_window[:].bitcast(I32), x_words[0].rearrange("p n t -> p (n t)").bitcast(I32))
 
         warm = keep.tile([P, 2], F32, name="warm")
         nc.vector.memset(warm[:, 0:1], 0.0)
         nc.scalar.activation(warm[:, 1:2], warm[:, 0:1], GELU)
 
-        x_plane = keep.tile([P, EARLY_PLACES], U8, name="x_plane", align_bytes=64)
+        x_plane = keep.tile([P, EARLY_PLACES], U8, name="x_plane", align_bytes=ALIGN)
         nc.vector.memset(x_plane[:].bitcast(I32), 0)
-        w2_plane = keep.tile([P, N], U8, name="w2_plane", align_bytes=64)
+        w2_plane = keep.tile([P, N], U8, name="w2_plane", align_bytes=ALIGN)
         nc.vector.memset(w2_plane[:].bitcast(I32), 0)
 
-        early_scales = keep.tile([P, EARLY_PLACES], U8, name="early_scales", align_bytes=64)
+        early_scales = keep.tile([P, EARLY_PLACES], U8, name="early_scales", align_bytes=ALIGN)
         nc.vector.tensor_copy(early_scales[:], scale_window[:].indirect(entries(0, EARLY_PLACES)))
         for q in range(QUADRANTS):
             nc.sync.dma_start(x_plane[32 * q : 32 * q + 4, :].bitcast(I32), early_scales[32 * q : 32 * q + 32 : 8, :].bitcast(I32))
-        late_scales = keep.tile([P, S - EARLY_PLACES], U8, name="late_scales", align_bytes=64)
+        late_scales = keep.tile([P, S - EARLY_PLACES], U8, name="late_scales", align_bytes=ALIGN)
         nc.vector.tensor_copy(late_scales[:], scale_window[:].indirect(entries(EARLY_PLACES, S)))
 
-        w1_grouped = keep.tile([P, H * PACK], BF16, name="w1_grouped", align_bytes=64)
+        w1_grouped = keep.tile([P, H * PACK], BF16, name="w1_grouped", align_bytes=ALIGN)
         groups = HALF // PACK
         nc.scalar.copy(
             w1_grouped[:].rearrange("p (t m j) -> p m j t", t=PACK, j=PACK)[:, 0:groups],
@@ -91,8 +92,8 @@ def tile_picked_phmlp_gelu_p_kernel(tc, x_words, x_scales, w1, w2_words, w2_scal
         raw_view = w1_raw[1][:].rearrange("p j (m u e) -> p u m j e", u=2, e=2)
         for pair in range(2):
             nc.scalar.copy(grouped_view[:, pair, groups:P], raw_view[:, pair])
-        w1_codes = keep.tile([P, H], U32, name="w1_codes", align_bytes=64)
-        w1_plane = keep.tile([P, H], U8, name="w1_plane", align_bytes=64)
+        w1_codes = keep.tile([P, H], U32, name="w1_codes", align_bytes=ALIGN)
+        w1_plane = keep.tile([P, H], U8, name="w1_plane", align_bytes=ALIGN)
         for pair in range(2):
             nc.vector.quantize_mx(
                 out=w1_codes[:, pair * HALF : (pair + 1) * HALF].bitcast(FP8X4),
@@ -100,12 +101,12 @@ def tile_picked_phmlp_gelu_p_kernel(tc, x_words, x_scales, w1, w2_words, w2_scal
                 in_=w1_grouped[:, pair * HALF * PACK : (pair + 1) * HALF * PACK],
             )
 
-        late_plane = keep.tile([P, S - EARLY_PLACES], U8, name="w1_raw1", align_bytes=64)
+        late_plane = keep.tile([P, S - EARLY_PLACES], U8, name="w1_raw1", align_bytes=ALIGN)
         nc.vector.tensor_copy(late_plane[:].bitcast(I32), late_scales[:].bitcast(I32))
         for row in range(1, PLANE_ROWS):
             nc.sync.dma_start(late_plane[row:P:32, :].bitcast(I32), late_scales[8 * row : P : 32, :].bitcast(I32))
 
-        w2_codes = keep.tile([P, N], U32, name="w2_codes", align_bytes=64)
+        w2_codes = keep.tile([P, N], U32, name="w2_codes", align_bytes=ALIGN)
         nc.sync.dma_start(w2_codes[:].bitcast(I32), w2_words[0].rearrange("p n t -> p (n t)").bitcast(I32))
         for q in range(QUADRANTS):
             nc.sync.dma_start(w2_plane[32 * q : 32 * q + 4, :].bitcast(I32), w2_scales[0, 4 * q : 4 * q + 4, :].bitcast(I32))
@@ -122,7 +123,7 @@ def tile_picked_phmlp_gelu_p_kernel(tc, x_words, x_scales, w1, w2_words, w2_scal
                 stop=True,
             )
 
-        picked_words = keep.tile([P, S], U32, name="picked_words", align_bytes=64)
+        picked_words = keep.tile([P, S], U32, name="picked_words", align_bytes=ALIGN)
         gathered = 0
         for width in WORD_GATHERS:
             nc.vector.tensor_copy(picked_words[:, gathered : gathered + width], word_window[:].indirect(entries(gathered, gathered + width)))
@@ -145,13 +146,13 @@ def tile_picked_phmlp_gelu_p_kernel(tc, x_words, x_scales, w1, w2_words, w2_scal
             return pre
 
         def gelu(pre, first, last, name):
-            h_values = keep.tile([P, (last - first) * PACK], BF16, name=name, align_bytes=64)
+            h_values = keep.tile([P, (last - first) * PACK], BF16, name=name, align_bytes=ALIGN)
             nc.scalar.activation(h_values[:].rearrange("p (n t) -> p n t", t=PACK), pre[:, :, first:last].rearrange("p t n -> p n t"), GELU)
             return h_values
 
         def quantise(h_values, width, name, turn):
-            h_codes = keep.tile([P, width], U32, name=name, align_bytes=64)
-            h_plane = keep.tile([P, width], U8, name=f"h_plane{turn % SLOTS}", align_bytes=64)
+            h_codes = keep.tile([P, width], U32, name=name, align_bytes=ALIGN)
+            h_plane = keep.tile([P, width], U8, name=f"h_plane{turn % SLOTS}", align_bytes=ALIGN)
             nc.vector.quantize_mx(out=h_codes[:].bitcast(FP8X4), scales=h_plane[:], in_=h_values[:])
             return h_codes, h_plane
 
@@ -169,7 +170,7 @@ def tile_picked_phmlp_gelu_p_kernel(tc, x_words, x_scales, w1, w2_words, w2_scal
         out_rows = out.rearrange("(h p) n -> p h n", p=P)
         staged = {}
         for first, last in STORE_GROUPS:
-            group = keep.tile([P, 2, (last - first) * STEP], F32, name=f"result{first}", align_bytes=64)
+            group = keep.tile([P, 2, (last - first) * STEP], F32, name=f"result{first}", align_bytes=ALIGN)
             for step in range(first, last):
                 staged[step] = (group, first, last)
 

@@ -28,7 +28,7 @@ BANKS = 8
 LEAD = 6
 LAG = 2
 SLOTS = LAG + 1
-EARLY_PLACES = S // 2
+EARLY_PLACES = 384
 WORD_GATHERS = (256, 256, 512)
 STORE_GROUPS = ((0, 2), (2, 4), (4, 5), (5, 6), (6, 7), (7, 8))
 SPLIT_FROM = 5
@@ -82,26 +82,23 @@ def tile_picked_phmlp_gelu_p_kernel(tc, x_words, x_scales, w1, w2_words, w2_scal
         late_scales = keep.tile([P, S - EARLY_PLACES], U8, name="late_scales", align_bytes=ALIGN)
         nc.vector.tensor_copy(late_scales[:], scale_window[:].indirect(entries(EARLY_PLACES, S)))
 
-        w1_grouped = keep.tile([P, H * PACK], BF16, name="w1_grouped", align_bytes=ALIGN)
+        w1_grouped = [keep.tile([P, HALF * PACK], BF16, name=f"w1_grouped{pair}", align_bytes=ALIGN) for pair in range(2)]
         groups = HALF // PACK
-        nc.scalar.copy(
-            w1_grouped[:].rearrange("p (t m j) -> p m j t", t=PACK, j=PACK)[:, 0:groups],
-            w1_raw[0][:].rearrange("p j (m t) -> p m j t", t=PACK),
-        )
-        grouped_view = w1_grouped[:].rearrange("p (u e m j) -> p u m j e", u=2, e=2, j=PACK)
-        raw_view = w1_raw[1][:].rearrange("p j (m u e) -> p u m j e", u=2, e=2)
-        for pair in range(2):
-            nc.scalar.copy(grouped_view[:, pair, groups:P], raw_view[:, pair])
+        for half in range(2):
+            raw_view = w1_raw[half][:].rearrange("p j (m u e) -> p u m j e", u=2, e=2)
+            for pair in range(2):
+                grouped_view = w1_grouped[pair][:].rearrange("p (e m j) -> p m j e", e=2, j=PACK)
+                nc.scalar.copy(grouped_view[:, half * groups : (half + 1) * groups], raw_view[:, pair])
         w1_codes = keep.tile([P, H], U32, name="w1_codes", align_bytes=ALIGN)
         w1_plane = keep.tile([P, H], U8, name="w1_plane", align_bytes=ALIGN)
         for pair in range(2):
             nc.vector.quantize_mx(
                 out=w1_codes[:, pair * HALF : (pair + 1) * HALF].bitcast(FP8X4),
                 scales=w1_plane[:, pair * HALF : (pair + 1) * HALF],
-                in_=w1_grouped[:, pair * HALF * PACK : (pair + 1) * HALF * PACK],
+                in_=w1_grouped[pair][:],
             )
 
-        late_plane = keep.tile([P, S - EARLY_PLACES], U8, name="w1_raw1", align_bytes=ALIGN)
+        late_plane = keep.tile([P, S - EARLY_PLACES], U8, name="w1_grouped0", align_bytes=ALIGN)
         nc.vector.tensor_copy(late_plane[:].bitcast(I32), late_scales[:].bitcast(I32))
         for row in range(1, PLANE_ROWS):
             nc.sync.dma_start(late_plane[row:P:32, :].bitcast(I32), late_scales[8 * row : P : 32, :].bitcast(I32))

@@ -28,9 +28,10 @@ BANKS = 8
 LEAD = 6
 LAG = 2
 SLOTS = LAG + 1
-EARLY_PLACES = 384
+EARLY_PLACES = 256
+X_FIRST = 1792
 WORD_GATHERS = (256, 256, 512)
-STORE_GROUPS = ((0, 2), (2, 4), (4, 5), (5, 6), (6, 7), (7, 8))
+STORE_GROUPS = ((0, 3), (3, 5), (5, 6), (6, 7), (7, 8))
 SPLIT_FROM = 5
 SPLIT_BANKS = ((3, 5), (4, 6))
 PART_BANKS = ((0, 1), (2, 7))
@@ -64,7 +65,8 @@ def tile_picked_phmlp_gelu_p_kernel(tc, x_words, x_scales, w1, w2_words, w2_scal
         nc.sync.dma_start(w1_raw[0][:, LEAD_ROWS:PACK, :], w1_rows[:, LEAD_ROWS:PACK, 0:HALF])
         nc.sync.dma_start(w1_raw[1][:], w1_rows[:, :, HALF:H])
         word_window = keep.tile([P, T], U32, name="word_window", align_bytes=ALIGN)
-        nc.sync.dma_start(word_window[:].bitcast(I32), x_words[0].rearrange("p n t -> p (n t)").bitcast(I32))
+        x_rows = x_words[0].rearrange("p n t -> p (n t)").bitcast(I32)
+        nc.sync.dma_start(word_window[:, 0:X_FIRST].bitcast(I32), x_rows[:, 0:X_FIRST])
 
         warm = keep.tile([P, 2], F32, name="warm")
         nc.vector.memset(warm[:, 0:1], 0.0)
@@ -79,6 +81,7 @@ def tile_picked_phmlp_gelu_p_kernel(tc, x_words, x_scales, w1, w2_words, w2_scal
         nc.vector.tensor_copy(early_scales[:], scale_window[:].indirect(entries(0, EARLY_PLACES)))
         for q in range(QUADRANTS):
             nc.sync.dma_start(x_plane[32 * q : 32 * q + 4, :].bitcast(I32), early_scales[32 * q : 32 * q + 32 : 8, :].bitcast(I32))
+        nc.sync.dma_start(word_window[:, X_FIRST:T].bitcast(I32), x_rows[:, X_FIRST:T])
         late_scales = keep.tile([P, S - EARLY_PLACES], U8, name="late_scales", align_bytes=ALIGN)
         nc.vector.tensor_copy(late_scales[:], scale_window[:].indirect(entries(EARLY_PLACES, S)))
 

from contextlib import ExitStack

import concourse.mybir as mybir

K, T, S, H, N = 512, 2048, 1024, 512, 256
FLOPS = 2 * S * (K * H + H * N)

F32 = mybir.dt.float32
BF16 = mybir.dt.bfloat16
I32 = mybir.dt.int32
U32 = mybir.dt.uint32
U16 = mybir.dt.uint16
U8 = mybir.dt.uint8
FP8X4 = mybir.dt.float8_e4m3fn_x4
GELU = mybir.ActivationFunctionType.Gelu_apprx_tanh

P = 128
ALIGN = 256
PACK = 4
QUADRANTS = 4
PLANE_ROWS = 4
LIST_ROWS = 16
STEP = 128
STEPS = S // STEP
HALF = H // 2
LEAD_ROWS = 3
BANKS = 8
LEAD = 6
LAG = 2
SLOTS = LAG + 1
EARLY_PLACES = 256
X_FIRST = 1792
WORD_GATHERS = (256, 256, 512)
STORE_GROUPS = ((0, 3), (3, 5), (5, 6), (6, 7), (7, 8))
SPLIT_FROM = 5
SPLIT_BANKS = ((3, 5), (4, 6))
PART_BANKS = ((0, 1), (2, 7))
TENSOR_WARM_UPS = (128, 128, 128, 128, 512)
WARM_UP_ROWS = 32


def tile_picked_phmlp_gelu_p_kernel(tc, x_words, x_scales, w1, w2_words, w2_scales, offs, out):
    nc = tc.nc
    with ExitStack() as ctx:
        keep = ctx.enter_context(tc.tile_pool(name="keep", bufs=1))
        psum = ctx.enter_context(tc.psum_pool(name="psum", bufs=1))

        def bank(number, *shape):
            return psum.tile([P, *shape], F32, name=f"bank{number}")

        offsets = keep.tile([P, S // LIST_ROWS], U16, name="offsets", align_bytes=ALIGN)

        def entries(first, last):
            return offsets[:, first // LIST_ROWS : last // LIST_ROWS]

        w1_rows = w1.rearrange("(p j) c -> p j c", j=PACK)
        w1_raw = [keep.tile([P, PACK, HALF], F32, name=f"w1_raw{half}", align_bytes=ALIGN) for half in range(2)]
        nc.sync.dma_start(w1_raw[0][:, 0:LEAD_ROWS, :], w1_rows[:, 0:LEAD_ROWS, 0:HALF])
        nc.sync.dma_start(offsets[:], offs)

        scale_window = keep.tile([P, T], U8, name="scale_window", align_bytes=ALIGN)
        nc.vector.memset(scale_window[:].bitcast(I32), 0)
        nc.sync.dma_start(scale_window[0:P:8, :].bitcast(I32), x_scales[0].bitcast(I32))

        nc.sync.dma_start(w1_raw[0][:, LEAD_ROWS:PACK, :], w1_rows[:, LEAD_ROWS:PACK, 0:HALF])
        nc.sync.dma_start(w1_raw[1][:], w1_rows[:, :, HALF:H])
        word_window = keep.tile([P, T], U32, name="word_window", align_bytes=ALIGN)
        x_rows = x_words[0].rearrange("p n t -> p (n t)").bitcast(I32)
        nc.sync.dma_start(word_window[:, 0:X_FIRST].bitcast(I32), x_rows[:, 0:X_FIRST])

        warm = keep.tile([P, 2], F32, name="warm")
        nc.vector.memset(warm[:, 0:1], 0.0)
        nc.scalar.activation(warm[:, 1:2], warm[:, 0:1], GELU)

        x_plane = keep.tile([P, EARLY_PLACES], U8, name="x_plane", align_bytes=ALIGN)
        nc.vector.memset(x_plane[:].bitcast(I32), 0)
        w2_plane = keep.tile([P, N], U8, name="w2_plane", align_bytes=ALIGN)
        nc.vector.memset(w2_plane[:].bitcast(I32), 0)

        early_scales = keep.tile([P, EARLY_PLACES], U8, name="early_scales", align_bytes=ALIGN)
        nc.vector.tensor_copy(early_scales[:], scale_window[:].indirect(entries(0, EARLY_PLACES)))
        for q in range(QUADRANTS):
            nc.sync.dma_start(x_plane[32 * q : 32 * q + 4, :].bitcast(I32), early_scales[32 * q : 32 * q + 32 : 8, :].bitcast(I32))
        nc.sync.dma_start(word_window[:, X_FIRST:T].bitcast(I32), x_rows[:, X_FIRST:T])
        late_scales = keep.tile([P, S - EARLY_PLACES], U8, name="late_scales", align_bytes=ALIGN)
        nc.vector.tensor_copy(late_scales[:], scale_window[:].indirect(entries(EARLY_PLACES, S)))

        w1_grouped = [keep.tile([P, HALF * PACK], BF16, name=f"w1_grouped{pair}", align_bytes=ALIGN) for pair in range(2)]
        groups = HALF // PACK
        for half in range(2):
            raw_view = w1_raw[half][:].rearrange("p j (m u e) -> p u m j e", u=2, e=2)
            for pair in range(2):
                grouped_view = w1_grouped[pair][:].rearrange("p (e m j) -> p m j e", e=2, j=PACK)
                nc.scalar.copy(grouped_view[:, half * groups : (half + 1) * groups], raw_view[:, pair])
        w1_codes = keep.tile([P, H], U32, name="w1_codes", align_bytes=ALIGN)
        w1_plane = keep.tile([P, H], U8, name="w1_plane", align_bytes=ALIGN)
        for pair in range(2):
            nc.vector.quantize_mx(
                out=w1_codes[:, pair * HALF : (pair + 1) * HALF].bitcast(FP8X4),
                scales=w1_plane[:, pair * HALF : (pair + 1) * HALF],
                in_=w1_grouped[pair][:],
            )

        late_plane = keep.tile([P, S - EARLY_PLACES], U8, name="w1_grouped0", align_bytes=ALIGN)
        nc.vector.tensor_copy(late_plane[:].bitcast(I32), late_scales[:].bitcast(I32))
        for row in range(1, PLANE_ROWS):
            nc.sync.dma_start(late_plane[row:P:32, :].bitcast(I32), late_scales[8 * row : P : 32, :].bitcast(I32))

        w2_codes = keep.tile([P, N], U32, name="w2_codes", align_bytes=ALIGN)
        nc.sync.dma_start(w2_codes[:].bitcast(I32), w2_words[0].rearrange("p n t -> p (n t)").bitcast(I32))
        for q in range(QUADRANTS):
            nc.sync.dma_start(w2_plane[32 * q : 32 * q + 4, :].bitcast(I32), w2_scales[0, 4 * q : 4 * q + 4, :].bitcast(I32))

        heat = psum.tile([WARM_UP_ROWS, H], F32, name=f"bank{BANKS - 1}")
        for width in TENSOR_WARM_UPS:
            nc.tensor.matmul_mx(
                out=heat[:, 0:width],
                lhsT=w1_codes[:, 0:WARM_UP_ROWS].bitcast(FP8X4),
                lhsT_scale=w1_plane[:, 0:WARM_UP_ROWS],
                rhs=w1_codes[:, 0:width].bitcast(FP8X4),
                rhs_scale=w1_plane[:, 0:width],
                start=True,
                stop=True,
            )

        picked_words = keep.tile([P, S], U32, name="picked_words", align_bytes=ALIGN)
        gathered = 0
        for width in WORD_GATHERS:
            nc.vector.tensor_copy(picked_words[:, gathered : gathered + width], word_window[:].indirect(entries(gathered, gathered + width)))
            gathered = gathered + width

        def first_product(step):
            cols = slice(step * STEP, (step + 1) * STEP)
            plane = x_plane[:, cols] if cols.start < EARLY_PLACES else late_plane[:, cols.start - EARLY_PLACES : cols.stop - EARLY_PLACES]
            pre = bank(step, PACK, STEP)
            for t in range(PACK):
                nc.tensor.matmul_mx(
                    out=pre[:, t, :],
                    lhsT=w1_codes[:, t * P : (t + 1) * P].bitcast(FP8X4),
                    lhsT_scale=w1_plane[:, t * P : (t + 1) * P],
                    rhs=picked_words[:, cols].bitcast(FP8X4),
                    rhs_scale=plane,
                    start=True,
                    stop=True,
                )
            return pre

        def gelu(pre, first, last, name):
            h_values = keep.tile([P, (last - first) * PACK], BF16, name=name, align_bytes=ALIGN)
            nc.scalar.activation(h_values[:].rearrange("p (n t) -> p n t", t=PACK), pre[:, :, first:last].rearrange("p t n -> p n t"), GELU)
            return h_values

        def quantise(h_values, width, name, turn):
            h_codes = keep.tile([P, width], U32, name=name, align_bytes=ALIGN)
            h_plane = keep.tile([P, width], U8, name=f"h_plane{turn % SLOTS}", align_bytes=ALIGN)
            nc.vector.quantize_mx(out=h_codes[:].bitcast(FP8X4), scales=h_plane[:], in_=h_values[:])
            return h_codes, h_plane

        def second_product(target, half, h_codes, h_plane):
            nc.tensor.matmul_mx(
                out=target,
                lhsT=w2_codes[:, half * P : (half + 1) * P].bitcast(FP8X4),
                lhsT_scale=w2_plane[:, half * P : (half + 1) * P],
                rhs=h_codes[:].bitcast(FP8X4),
                rhs_scale=h_plane[:],
                start=True,
                stop=True,
            )

        out_rows = out.rearrange("(h p) n -> p h n", p=P)
        staged = {}
        for first, last in STORE_GROUPS:
            group = keep.tile([P, 2, (last - first) * STEP], F32, name=f"result{first}", align_bytes=ALIGN)
            for step in range(first, last):
                staged[step] = (group, first, last)

        def store_if_complete(step):
            group, first, last = staged[step]
            if step == last - 1:
                nc.sync.dma_start(out_rows[:, :, first * STEP : last * STEP], group[:])

        hidden = {}
        for step in range(LEAD):
            hidden[step] = gelu(first_product(step), 0, STEP, f"hidden{step}")

        part = STEP // 2
        last_step = STEPS - 1
        acc = {}
        for step in range(last_step):
            codes = quantise(hidden[step], STEP, f"h_codes{step}", step)
            if step < SPLIT_FROM:
                acc[step] = bank((LEAD + step) % BANKS, 2, STEP)
                targets = [acc[step][:, half, :] for half in range(2)]
            else:
                acc[step] = [bank(number, STEP) for number in SPLIT_BANKS[step - SPLIT_FROM]]
                targets = [tile[:] for tile in acc[step]]
            for half in range(2):
                second_product(targets[half], half, *codes)
            done = step - LAG
            if done >= 0:
                group, first, last = staged[done]
                nc.vector.tensor_copy(group[:, :, (done - first) * STEP : (done - first + 1) * STEP], acc[done][:])
                store_if_complete(done)
            if done == 0:
                hidden[LEAD] = gelu(first_product(LEAD), 0, STEP, f"hidden{LEAD}")
            if done == 1:
                pre = first_product(last_step)
                parts = [gelu(pre, 0, part, "hidden_part0"), gelu(pre, part, STEP, "hidden_part1")]

        part_codes = [quantise(parts[number], part, f"h_codes_part{number}", last_step + number) for number in range(2)]
        engine_copies = (nc.scalar.copy, nc.vector.tensor_copy)
        for step in range(SPLIT_FROM, last_step):
            for half, engine_copy in enumerate(engine_copies):
                engine_copy(staged[step][0][:, half, :], acc[step][half][:])
            store_if_complete(step)
        for number, codes in enumerate(part_codes):
            for half, engine_copy in enumerate(engine_copies):
                part_acc = bank(PART_BANKS[number][half], part)
                second_product(part_acc[:], half, *codes)
                engine_copy(staged[last_step][0][:, half, number * part : (number + 1) * part], part_acc[:])
        store_if_complete(last_step)
